import numpy as np
import ml_dtypes


def mxq(x, axis, fmt="e4m3"):
    dtype, down = {"e4m3": (ml_dtypes.float8_e4m3fn, 7), "e5m2": (ml_dtypes.float8_e5m2, 14)}[fmt]
    v = np.moveaxis(np.asarray(x, np.float32).astype(ml_dtypes.bfloat16).astype(np.float64), axis, -1)
    blocks = v.reshape(v.shape[:-1] + (-1, 32))
    amax = np.abs(blocks).max(-1, keepdims=True)
    byte = np.maximum(np.where(amax > 0, np.frexp(amax)[1] - 1 + 127, 0) - down, 1)
    scale = np.exp2(byte - 127.0)
    codes = (blocks / scale).astype(np.float32).astype(dtype).astype(np.float64)
    return np.moveaxis((codes * scale).reshape(v.shape), -1, axis)


WIDE = False


def mx_kscale(k):
    if not WIDE:
        return np.ones(k)
    levels = np.array([10, -10, 5, -5, 0])
    if k % 512:
        return np.exp2(np.random.permutation(np.resize(levels, k // 32))).repeat(32)
    a = np.empty((k // 512, 16))
    for p in range(k // 512):
        a[p, :8] = np.random.permutation(np.resize(levels, 8))
        for g in range(8):
            far = levels[np.abs(levels - a[p, g]) >= 10]
            a[p, g + 8] = far[np.random.randint(len(far))]
    return np.exp2(a.ravel()).repeat(32)


def f64(x):
    return np.asarray(x).astype(np.float64)


def striped8(idx):
    return np.concatenate([x.reshape(-1, 16).T for x in idx]).astype(np.uint16)


def runs(offs, k):
    lists = np.stack([offs[16 * r : 16 * r + 16].T.reshape(-1) for r in range(8)]).astype(np.int64)
    return lists[np.arange(k) % 512 // 64]


def pack_weight(w):
    k, n = w.shape
    w = f64(np.asarray(w, np.float32).astype(ml_dtypes.bfloat16)).reshape(k // 32, 32, n)
    amax = np.abs(w).max(1)
    byte = np.clip(np.where(amax > 0, np.frexp(amax)[1] - 1 + 127 - 7, 1), 1, 254)
    scaled = (w * np.exp2(127.0 - byte)[:, None, :]).reshape(k, n).astype(np.float32)
    words = np.ascontiguousarray(scaled.reshape(k // 512, 128, 4, n).transpose(0, 1, 3, 2)).astype(ml_dtypes.float8_e4m3fn).view(np.uint8)
    return words, np.ascontiguousarray(byte.astype(np.uint8).reshape(k // 512, 16, n))


def unpack_weight(words, scales):
    g, p, n, _ = words.shape
    vals = np.ascontiguousarray(words).view(ml_dtypes.float8_e4m3fn).astype(np.float64) * np.repeat(np.exp2(scales.astype(np.float64) - 127.0), 8, axis=1)[..., None]
    return vals.transpose(0, 1, 3, 2).reshape(g * 512, n)

def planes(y):
    n, m = y.shape
    v = y.astype(np.float32).astype(ml_dtypes.bfloat16).astype(np.float64).reshape(n // 32, 32, m)
    top = np.abs(v).max(1)
    byte = np.clip(np.where(top > 0, np.frexp(top)[1] - 1 + 127 - 7, 1), 1, 254)
    codes = (v * np.exp2(127.0 - byte)[:, None, :]).reshape(n, m).astype(np.float32).astype(ml_dtypes.float8_e4m3fn).view(np.uint8)
    words = codes.reshape(n // 512, 128, 4, m).transpose(0, 1, 3, 2)
    return np.ascontiguousarray(words), np.ascontiguousarray(byte.astype(np.uint8).reshape(n // 512, 16, m))


K, T, S, H = 512, 2048, 512, 512


def setup_inputs():
    n = np.random.standard_normal
    s = mx_kscale(K)[:, None]
    u = mx_kscale(H)
    packed_xT = pack_weight(n((K, T)) * s)
    packed_w1 = pack_weight(n((K, H)) / np.sqrt(2 * K) / s)
    packed_w3 = pack_weight(n((H, H)) / np.sqrt(2 * H) / u[:, None])
    return {
        "x_words": packed_xT[0],
        "x_scales": packed_xT[1],
        "w1_words": packed_w1[0],
        "w1_scales": packed_w1[1],
        "w2": (n((K, H)) / np.sqrt(K) / s * u).astype(np.float32),
        "w3_words": packed_w3[0],
        "w3_scales": packed_w3[1],
        "offs": striped8(np.stack([np.random.permutation(T)[:S] for _ in range(8)])),
    }


def reference(x_words, x_scales, w1_words, w1_scales, w2, w3_words, w3_scales, offs):
    xq = unpack_weight(x_words, x_scales)[np.arange(K)[:, None], runs(offs, K)]
    h = mxq(f64(w2), 0, "e4m3").T @ xq
    out_0 = unpack_weight(w1_words, w1_scales).T @ xq + unpack_weight(w3_words, w3_scales).T @ mxq(h, 0, "e4m3")
    return (out_0,) + planes(out_0)

@@ -1,0 +1,161 @@
+from contextlib import ExitStack
+
+import concourse.mybir as mybir
+
+F32 = mybir.dt.float32
+BF16 = mybir.dt.bfloat16
+I32 = mybir.dt.int32
+U32 = mybir.dt.uint32
+U16 = mybir.dt.uint16
+U8 = mybir.dt.uint8
+FP8X4 = mybir.dt.float8_e4m3fn_x4
+
+P = 128
+PACK = 4
+T = 2048
+S = 512
+H = 512
+HALF = 256
+CHUNK = 128
+FLOPS = 3 * 2 * 512 * 512 * 512
+
+
+def tile_picked_phlora_none_po_kernel(
+    tc, x_words, x_scales, w1_words, w1_scales, w2, w3_words, w3_scales, offs, out_0, out_1, out_2
+):
+    nc = tc.nc
+
+    def words(dram):
+        return dram[0].rearrange("p c t -> p (c t)").bitcast(I32)
+
+    with ExitStack() as ctx:
+        keep = ctx.enter_context(tc.tile_pool(name="keep", bufs=1))
+        psum = ctx.enter_context(tc.psum_pool(name="psum", bufs=1))
+
+        def tile(name, cols, dtype, tag=None):
+            return keep.tile([P, cols], dtype, name=name, tag=tag or name, align_bytes=64)
+
+        offsets = keep.tile([P, S // 16], U16, name="offsets")
+        xs_win = tile("xs_win", T, U8, tag="xs_then_w1")
+        ws_raw = tile("ws_raw", 2 * H, U8, tag="ws_then_w3")
+        scales = tile("scales", S + 2 * H, U8)
+        x_win = tile("x_win", T, U32)
+        w2_raw = tile("w2_raw", PACK * H, F32)
+
+        nc.vector.memset(xs_win[:].bitcast(I32), 0)
+        nc.vector.memset(ws_raw[:].bitcast(I32), 0)
+
+        nc.sync.dma_start(offsets[:], offs)
+        nc.sync.dma_start(out=xs_win[0:P:8, :].bitcast(I32), in_=x_scales[0].bitcast(I32))
+        nc.sync.dma_start(out=ws_raw[0:P:8, 0:H].bitcast(I32), in_=w1_scales[0].bitcast(I32))
+        nc.sync.dma_start(out=ws_raw[0:P:8, H : 2 * H].bitcast(I32), in_=w3_scales[0].bitcast(I32))
+        nc.scalar.dma_start(out=w2_raw[:], in_=w2.rearrange("(p j) c -> p (j c)", j=PACK))
+        nc.scalar.dma_start(out=x_win[:].bitcast(I32), in_=words(x_words))
+
+        xs_got = tile("xs_got", S, U8)
+        nc.vector.tensor_copy(xs_got[:], xs_win[:].indirect(offsets[:]))
+        w1_raw = tile("w1_raw", H, I32, tag="xs_then_w1")
+        nc.scalar.dma_start(out=w1_raw[:], in_=words(w1_words))
+        nc.vector.tensor_copy(out=scales[:, 0:S].bitcast(I32), in_=xs_got[:].bitcast(I32))
+        nc.vector.tensor_copy(
+            out=scales[:, S:].rearrange("p (w t m) -> p w t m", w=2, t=PACK),
+            in_=ws_raw[:].rearrange("p (w m t) -> p w t m", w=2, t=PACK),
+        )
+        for j in range(1, PACK):
+            nc.sync.dma_start(out=scales[j:P:32, :].bitcast(I32), in_=scales[8 * j : P : 32, :].bitcast(I32))
+        w3_raw = tile("w3_raw", H, I32, tag="ws_then_w3")
+        nc.sync.dma_start(out=w3_raw[:], in_=words(w3_words))
+
+        w2_bf = tile("w2_bf", PACK * H, BF16)
+        w2_codes = tile("w2_codes", H, U32)
+        w2_plane = tile("w2_plane", H, U8)
+        src = w2_raw[:].rearrange("p (j m t) -> p m j t", j=PACK, t=PACK)
+        dst = w2_bf[:].rearrange("p (t m j) -> p m j t", j=PACK, t=PACK)
+        nc.scalar.copy(out=dst[:, 0:64], in_=src[:, 0:64])
+        nc.vector.tensor_copy(out=dst[:, 64:128], in_=src[:, 64:128])
+        nc.vector.quantize_mx(out=w2_codes[:].bitcast(FP8X4), scales=w2_plane[:], in_=w2_bf[:])
+
+        x_got = [tile("x_got%d" % a, HALF, U32) for a in range(2)]
+        for a in range(2):
+            nc.vector.tensor_copy(x_got[a][:], x_win[:].indirect(offsets[:, 16 * a : 16 * (a + 1)]))
+
+        w_codes = []
+        for name, raw in (("w1_codes", w1_raw), ("w3_codes", w3_raw)):
+            dealt = tile(name, H, I32)
+            nc.vector.tensor_copy(
+                out=dealt[:].rearrange("p (t m) -> p m t", t=PACK), in_=raw[:].rearrange("p (m t) -> p m t", t=PACK)
+            )
+            w_codes.append(dealt)
+
+        h_codes = [tile("h_codes%d" % a, HALF, U32) for a in range(2)]
+        h_plane = [tile("h_plane%d" % a, HALF, U8) for a in range(2)]
+        for a in range(2):
+            h_bf = tile("h_bf%d" % a, PACK * HALF, BF16)
+            for c in range(2):
+                bank = psum.tile([P, PACK * CHUNK], F32, name="h_acc%d%d" % (a, c), tag="late%d" % (2 * a + c))
+                for t in range(PACK):
+                    nc.tensor.matmul_mx(
+                        out=bank[:, t * CHUNK : (t + 1) * CHUNK],
+                        lhsT=w2_codes[:, t * P : (t + 1) * P].bitcast(FP8X4),
+                        lhsT_scale=w2_plane[:, t * P : (t + 1) * P],
+                        rhs=x_got[a][:, c * CHUNK : (c + 1) * CHUNK].bitcast(FP8X4),
+                        rhs_scale=scales[:, a * HALF + c * CHUNK : a * HALF + (c + 1) * CHUNK],
+                        start=True,
+                        stop=True,
+                    )
+                piece = h_bf[:, c * PACK * CHUNK : (c + 1) * PACK * CHUNK].rearrange("p (n t) -> p n t", t=PACK)
+                sums = bank[:].rearrange("p (t n) -> p n t", t=PACK)
+                if (a, c) == (0, 1):
+                    nc.vector.tensor_copy(out=piece, in_=sums)
+                else:
+                    nc.scalar.copy(out=piece, in_=sums)
+            nc.vector.quantize_mx(out=h_codes[a][:].bitcast(FP8X4), scales=h_plane[a][:], in_=h_bf[:])
+
+        y_rows = out_0.rearrange("(p t) c -> p t c", t=PACK)
+        y_plane = tile("y_plane", S, U8)
+        for a in range(2):
+            cols = slice(a * HALF, (a + 1) * HALF)
+            banks = [
+                psum.tile([P, HALF], F32, name="y_acc%d%d" % (a, t), tag=("early%d" if a == 0 else "late%d") % t)
+                for t in range(PACK)
+            ]
+            for t in range(PACK):
+                nc.tensor.matmul_mx(
+                    out=banks[t][:],
+                    lhsT=w_codes[0][:, t * P : (t + 1) * P].bitcast(FP8X4),
+                    lhsT_scale=scales[:, S + t * P : S + (t + 1) * P],
+                    rhs=x_got[a][:].bitcast(FP8X4),
+                    rhs_scale=scales[:, cols],
+                    start=True,
+                    stop=False,
+                )
+            y = tile("y%d" % a, PACK * HALF, F32)
+            for t in range(PACK):
+                nc.tensor.matmul_mx(
+                    out=banks[t][:],
+                    lhsT=w_codes[1][:, t * P : (t + 1) * P].bitcast(FP8X4),
+                    lhsT_scale=scales[:, S + H + t * P : S + H + (t + 1) * P],
+                    rhs=h_codes[a][:].bitcast(FP8X4),
+                    rhs_scale=h_plane[a][:],
+                    start=False,
+                    stop=True,
+                )
+                if (a, t) in ((0, 1), (0, 3), (1, 3)):
+                    nc.vector.tensor_copy(out=y[:, t * HALF : (t + 1) * HALF], in_=banks[t][:])
+                else:
+                    nc.scalar.copy(out=y[:, t * HALF : (t + 1) * HALF], in_=banks[t][:])
+            nc.sync.dma_start(out=y_rows[:, :, cols], in_=y[:].rearrange("p (t c) -> p t c", t=PACK))
+            y_bf = tile("y_bf%d" % a, PACK * HALF, BF16)
+            y_codes = tile("y_codes%d" % a, HALF, U32)
+            dst = y_bf[:].rearrange("p (c i t) -> p c t i", i=4, t=PACK)
+            src = y[:].rearrange("p (t c i) -> p c t i", i=4, t=PACK)
+            share = (16, 20)[a]
+            nc.scalar.copy(out=dst[:, :share], in_=src[:, :share])
+            nc.vector.tensor_copy(out=dst[:, share:], in_=src[:, share:])
+            nc.vector.quantize_mx(out=y_codes[:].bitcast(FP8X4), scales=y_plane[:, cols], in_=y_bf[:])
+            nc.sync.dma_start(out=words(out_1)[:, cols], in_=y_codes[:].bitcast(I32))
+        for q in range(4):
+            queue = nc.sync if q % 2 == 0 else nc.scalar
+            queue.dma_start(
+                out=out_2[0][4 * q : 4 * q + 4, :].bitcast(I32), in_=y_plane[32 * q : 32 * q + 4, :].bitcast(I32)
+            )

@@ -17,6 +17,7 @@ S = 512
 H = 512
 HALF = 256
 CHUNK = 128
+X_HEAD = 512
 FLOPS = 3 * 2 * 512 * 512 * 512
 
 
@@ -36,124 +37,173 @@ def tile_picked_phlora_none_po_kernel(
             return keep.tile([P, cols], dtype, name=name, tag=tag or name, align_bytes=64)
 
         offsets = keep.tile([P, S // 16], U16, name="offsets")
-        xs_win = tile("xs_win", T, U8, tag="xs_then_w1")
-        ws_raw = tile("ws_raw", 2 * H, U8, tag="ws_then_w3")
+        xs_win = tile("xs_win", T, U8)
+        ws_raw = tile("ws_raw", 2 * H, U8)
         scales = tile("scales", S + 2 * H, U8)
-        x_win = tile("x_win", T, U32)
+        x_win = tile("x_win", T, U32, tag="x_then_w")
         w2_raw = tile("w2_raw", PACK * H, F32)
 
         nc.vector.memset(xs_win[:].bitcast(I32), 0)
-        nc.vector.memset(ws_raw[:].bitcast(I32), 0)
+
+        seed = tile("seed", 16, F32)
+        seed_bf = tile("seed_bf", 16, BF16)
+        nc.gpsimd.memset(seed[:], 0.0)
+        nc.scalar.copy(out=seed_bf[:], in_=seed[:])
 
         nc.sync.dma_start(offsets[:], offs)
+        w2_rows = w2.rearrange("(p j) c -> p (j c)", j=PACK)
+        nc.sync.dma_start(out=w2_raw[:, 0:H], in_=w2_rows[:, 0:H])
         nc.sync.dma_start(out=xs_win[0:P:8, :].bitcast(I32), in_=x_scales[0].bitcast(I32))
-        nc.sync.dma_start(out=ws_raw[0:P:8, 0:H].bitcast(I32), in_=w1_scales[0].bitcast(I32))
-        nc.sync.dma_start(out=ws_raw[0:P:8, H : 2 * H].bitcast(I32), in_=w3_scales[0].bitcast(I32))
-        nc.scalar.dma_start(out=w2_raw[:], in_=w2.rearrange("(p j) c -> p (j c)", j=PACK))
-        nc.scalar.dma_start(out=x_win[:].bitcast(I32), in_=words(x_words))
+        for w, rows in enumerate((w1_scales, w3_scales)):
+            nc.sync.dma_start(
+                out=ws_raw[:, w * H : (w + 1) * H].bitcast(I32),
+                in_=rows[0].bitcast(I32).unsqueeze(1).to_broadcast([16, 8, H // 4]),
+            )
+        nc.sync.dma_start(out=w2_raw[:, H:], in_=w2_rows[:, H:])
+        nc.sync.dma_start(out=x_win[:, 0:X_HEAD].bitcast(I32), in_=words(x_words)[:, 0:X_HEAD])
+        w1_head = tile("w1_head", P, I32)
+        nc.sync.dma_start(out=w1_head[:], in_=words(w1_words)[:, 0:P])
+        nc.sync.dma_start(out=x_win[:, X_HEAD:].bitcast(I32), in_=words(x_words)[:, X_HEAD:])
 
-        xs_got = tile("xs_got", S, U8)
+        xs_got = tile("xs_got", S, U8, tag="xs_then_w")
         nc.vector.tensor_copy(xs_got[:], xs_win[:].indirect(offsets[:]))
-        w1_raw = tile("w1_raw", H, I32, tag="xs_then_w1")
-        nc.scalar.dma_start(out=w1_raw[:], in_=words(w1_words))
-        nc.vector.tensor_copy(out=scales[:, 0:S].bitcast(I32), in_=xs_got[:].bitcast(I32))
         nc.vector.tensor_copy(
             out=scales[:, S:].rearrange("p (w t m) -> p w t m", w=2, t=PACK),
             in_=ws_raw[:].rearrange("p (w m t) -> p w t m", w=2, t=PACK),
         )
+        nc.vector.tensor_copy(out=scales[:, 0:S].bitcast(I32), in_=xs_got[:].bitcast(I32))
         for j in range(1, PACK):
             nc.sync.dma_start(out=scales[j:P:32, :].bitcast(I32), in_=scales[8 * j : P : 32, :].bitcast(I32))
-        w3_raw = tile("w3_raw", H, I32, tag="ws_then_w3")
-        nc.sync.dma_start(out=w3_raw[:], in_=words(w3_words))
+        warm = psum.tile([P, P], F32, name="warm", tag="early0")
+        for i in range(12):
+            nc.tensor.matmul_mx(
+                out=warm[:],
+                lhsT=w1_head[:].bitcast(FP8X4),
+                lhsT_scale=ws_raw[:, 0:P],
+                rhs=w1_head[:].bitcast(FP8X4),
+                rhs_scale=ws_raw[:, 0:P],
+                start=True,
+                stop=True,
+            )
+        w_raw = tile("w_raw", 2 * H, I32, tag="xs_then_w")
+        nc.sync.dma_start(out=w_raw[:, P:H], in_=words(w1_words)[:, P:H])
+        nc.sync.dma_start(out=w_raw[:, H:], in_=words(w3_words))
 
-        w2_bf = tile("w2_bf", PACK * H, BF16)
+        w2_bf = tile("w2_bf", PACK * H, BF16, tag="w2_then_x")
         w2_codes = tile("w2_codes", H, U32)
         w2_plane = tile("w2_plane", H, U8)
         src = w2_raw[:].rearrange("p (j m t) -> p m j t", j=PACK, t=PACK)
         dst = w2_bf[:].rearrange("p (t m j) -> p m j t", j=PACK, t=PACK)
-        nc.scalar.copy(out=dst[:, 0:64], in_=src[:, 0:64])
-        nc.vector.tensor_copy(out=dst[:, 64:128], in_=src[:, 64:128])
+        nc.scalar.copy(out=dst[:, 0:46], in_=src[:, 0:46])
+        nc.vector.tensor_copy(out=dst[:, 46:128], in_=src[:, 46:128])
         nc.vector.quantize_mx(out=w2_codes[:].bitcast(FP8X4), scales=w2_plane[:], in_=w2_bf[:])
 
-        x_got = [tile("x_got%d" % a, HALF, U32) for a in range(2)]
+        x_all = tile("x_all", S, U32, tag="w2_then_x")
+        x_got = [x_all[:, a * HALF : (a + 1) * HALF] for a in range(2)]
         for a in range(2):
-            nc.vector.tensor_copy(x_got[a][:], x_win[:].indirect(offsets[:, 16 * a : 16 * (a + 1)]))
+            nc.vector.tensor_copy(x_got[a], x_win[:].indirect(offsets[:, 16 * a : 16 * (a + 1)]))
 
-        w_codes = []
-        for name, raw in (("w1_codes", w1_raw), ("w3_codes", w3_raw)):
-            dealt = tile(name, H, I32)
+        w_dealt = tile("w_dealt", 2 * H, I32, tag="x_then_w")
+
+        def deal(w, source, first, count):
+            dealt = w_dealt[:, w * H : (w + 1) * H].rearrange("p (t m) -> p m t", t=PACK)
             nc.vector.tensor_copy(
-                out=dealt[:].rearrange("p (t m) -> p m t", t=PACK), in_=raw[:].rearrange("p (m t) -> p m t", t=PACK)
+                out=dealt[:, first // PACK : (first + count) // PACK, :],
+                in_=source.rearrange("p (m t) -> p m t", t=PACK),
             )
-            w_codes.append(dealt)
 
+        h_bf = [tile("h_bf%d" % a, PACK * HALF, BF16) for a in range(2)]
         h_codes = [tile("h_codes%d" % a, HALF, U32) for a in range(2)]
         h_plane = [tile("h_plane%d" % a, HALF, U8) for a in range(2)]
-        for a in range(2):
-            h_bf = tile("h_bf%d" % a, PACK * HALF, BF16)
-            for c in range(2):
-                bank = psum.tile([P, PACK * CHUNK], F32, name="h_acc%d%d" % (a, c), tag="late%d" % (2 * a + c))
-                for t in range(PACK):
-                    nc.tensor.matmul_mx(
-                        out=bank[:, t * CHUNK : (t + 1) * CHUNK],
-                        lhsT=w2_codes[:, t * P : (t + 1) * P].bitcast(FP8X4),
-                        lhsT_scale=w2_plane[:, t * P : (t + 1) * P],
-                        rhs=x_got[a][:, c * CHUNK : (c + 1) * CHUNK].bitcast(FP8X4),
-                        rhs_scale=scales[:, a * HALF + c * CHUNK : a * HALF + (c + 1) * CHUNK],
-                        start=True,
-                        stop=True,
-                    )
-                piece = h_bf[:, c * PACK * CHUNK : (c + 1) * PACK * CHUNK].rearrange("p (n t) -> p n t", t=PACK)
-                sums = bank[:].rearrange("p (t n) -> p n t", t=PACK)
-                if (a, c) == (0, 1):
-                    nc.vector.tensor_copy(out=piece, in_=sums)
-                else:
-                    nc.scalar.copy(out=piece, in_=sums)
-            nc.vector.quantize_mx(out=h_codes[a][:].bitcast(FP8X4), scales=h_plane[a][:], in_=h_bf[:])
+
+        def hidden(chunk, copy):
+            bank = psum.tile([P, PACK * CHUNK], F32, name="h_acc%d" % chunk, tag="late%d" % chunk)
+            cols = slice(chunk * CHUNK, (chunk + 1) * CHUNK)
+            for t in range(PACK):
+                nc.tensor.matmul_mx(
+                    out=bank[:, t * CHUNK : (t + 1) * CHUNK],
+                    lhsT=w2_codes[:, t * P : (t + 1) * P].bitcast(FP8X4),
+                    lhsT_scale=w2_plane[:, t * P : (t + 1) * P],
+                    rhs=x_all[:, cols].bitcast(FP8X4),
+                    rhs_scale=scales[:, cols],
+                    start=True,
+                    stop=True,
+                )
+            c = chunk % 2
+            copy(
+                out=h_bf[chunk // 2][:, c * PACK * CHUNK : (c + 1) * PACK * CHUNK].rearrange("p (n t) -> p n t", t=PACK),
+                in_=bank[:].rearrange("p (t n) -> p n t", t=PACK),
+            )
+
+        def quantise_hidden(a):
+            nc.vector.quantize_mx(out=h_codes[a][:].bitcast(FP8X4), scales=h_plane[a][:], in_=h_bf[a][:])
+
+        banks = {}
+
+        def first_term(a, t):
+            banks[a, t] = psum.tile([P, HALF], F32, name="y_acc%d%d" % (a, t), tag=("early%d", "late%d")[a] % t)
+            nc.tensor.matmul_mx(
+                out=banks[a, t][:],
+                lhsT=w_dealt[:, t * P : (t + 1) * P].bitcast(FP8X4),
+                lhsT_scale=scales[:, S + t * P : S + (t + 1) * P],
+                rhs=x_got[a].bitcast(FP8X4),
+                rhs_scale=scales[:, a * HALF : (a + 1) * HALF],
+                start=True,
+                stop=False,
+            )
+
+        y = [tile("y%d" % a, PACK * HALF, F32) for a in range(2)]
+
+        def second_term(a, t, copy):
+            nc.tensor.matmul_mx(
+                out=banks[a, t][:],
+                lhsT=w_dealt[:, H + t * P : H + (t + 1) * P].bitcast(FP8X4),
+                lhsT_scale=scales[:, S + H + t * P : S + H + (t + 1) * P],
+                rhs=h_codes[a][:].bitcast(FP8X4),
+                rhs_scale=h_plane[a][:],
+                start=False,
+                stop=True,
+            )
+            copy(out=y[a][:, t * HALF : (t + 1) * HALF], in_=banks[a, t][:])
 
         y_rows = out_0.rearrange("(p t) c -> p t c", t=PACK)
         y_plane = tile("y_plane", S, U8)
-        for a in range(2):
+
+        def hand_out(a, share):
             cols = slice(a * HALF, (a + 1) * HALF)
-            banks = [
-                psum.tile([P, HALF], F32, name="y_acc%d%d" % (a, t), tag=("early%d" if a == 0 else "late%d") % t)
-                for t in range(PACK)
-            ]
-            for t in range(PACK):
-                nc.tensor.matmul_mx(
-                    out=banks[t][:],
-                    lhsT=w_codes[0][:, t * P : (t + 1) * P].bitcast(FP8X4),
-                    lhsT_scale=scales[:, S + t * P : S + (t + 1) * P],
-                    rhs=x_got[a][:].bitcast(FP8X4),
-                    rhs_scale=scales[:, cols],
-                    start=True,
-                    stop=False,
-                )
-            y = tile("y%d" % a, PACK * HALF, F32)
-            for t in range(PACK):
-                nc.tensor.matmul_mx(
-                    out=banks[t][:],
-                    lhsT=w_codes[1][:, t * P : (t + 1) * P].bitcast(FP8X4),
-                    lhsT_scale=scales[:, S + H + t * P : S + H + (t + 1) * P],
-                    rhs=h_codes[a][:].bitcast(FP8X4),
-                    rhs_scale=h_plane[a][:],
-                    start=False,
-                    stop=True,
-                )
-                if (a, t) in ((0, 1), (0, 3), (1, 3)):
-                    nc.vector.tensor_copy(out=y[:, t * HALF : (t + 1) * HALF], in_=banks[t][:])
-                else:
-                    nc.scalar.copy(out=y[:, t * HALF : (t + 1) * HALF], in_=banks[t][:])
-            nc.sync.dma_start(out=y_rows[:, :, cols], in_=y[:].rearrange("p (t c) -> p t c", t=PACK))
+            nc.sync.dma_start(out=y_rows[:, :, cols], in_=y[a][:].rearrange("p (t c) -> p t c", t=PACK))
             y_bf = tile("y_bf%d" % a, PACK * HALF, BF16)
             y_codes = tile("y_codes%d" % a, HALF, U32)
             dst = y_bf[:].rearrange("p (c i t) -> p c t i", i=4, t=PACK)
-            src = y[:].rearrange("p (t c i) -> p c t i", i=4, t=PACK)
-            share = (16, 20)[a]
-            nc.scalar.copy(out=dst[:, :share], in_=src[:, :share])
+            src = y[a][:].rearrange("p (t c i) -> p c t i", i=4, t=PACK)
+            if share:
+                nc.scalar.copy(out=dst[:, :share], in_=src[:, :share])
             nc.vector.tensor_copy(out=dst[:, share:], in_=src[:, share:])
             nc.vector.quantize_mx(out=y_codes[:].bitcast(FP8X4), scales=y_plane[:, cols], in_=y_bf[:])
             nc.sync.dma_start(out=words(out_1)[:, cols], in_=y_codes[:].bitcast(I32))
+
+        on_scalar = nc.scalar.copy
+        on_vector = nc.vector.tensor_copy
+        hidden(0, on_scalar)
+        hidden(1, on_scalar)
+        deal(0, w1_head[:], 0, P)
+        deal(0, w_raw[:, P:H], P, H - P)
+        hidden(2, on_vector)
+        hidden(3, on_scalar)
+        deal(1, w_raw[:, H:], 0, H)
+        quantise_hidden(0)
+        quantise_hidden(1)
+        for t in range(PACK):
+            first_term(0, t)
+        for t in range(PACK - 1):
+            first_term(1, t)
+        for t in range(PACK):
+            second_term(0, t, (on_scalar, on_vector)[t % 2])
+        first_term(1, PACK - 1)
+        hand_out(0, 0)
+        for t in range(PACK):
+            second_term(1, t, on_scalar)
+        hand_out(1, 24)
         for q in range(4):
             queue = nc.sync if q % 2 == 0 else nc.scalar
             queue.dma_start(

@@ -44,6 +44,7 @@ def tile_picked_phlora_none_po_kernel(
         w2_raw = tile("w2_raw", PACK * H, F32)
 
         nc.vector.memset(xs_win[:].bitcast(I32), 0)
+        nc.vector.memset(ws_raw[:].bitcast(I32), 0)
 
         seed = tile("seed", 16, F32)
         seed_bf = tile("seed_bf", 16, BF16)
@@ -52,14 +53,11 @@ def tile_picked_phlora_none_po_kernel(
 
         nc.sync.dma_start(offsets[:], offs)
         w2_rows = w2.rearrange("(p j) c -> p (j c)", j=PACK)
-        nc.sync.dma_start(out=w2_raw[:, 0:H], in_=w2_rows[:, 0:H])
+        nc.sync.dma_start(out=w2_raw[:, 0 : 2 * H], in_=w2_rows[:, 0 : 2 * H])
         nc.sync.dma_start(out=xs_win[0:P:8, :].bitcast(I32), in_=x_scales[0].bitcast(I32))
         for w, rows in enumerate((w1_scales, w3_scales)):
-            nc.sync.dma_start(
-                out=ws_raw[:, w * H : (w + 1) * H].bitcast(I32),
-                in_=rows[0].bitcast(I32).unsqueeze(1).to_broadcast([16, 8, H // 4]),
-            )
-        nc.sync.dma_start(out=w2_raw[:, H:], in_=w2_rows[:, H:])
+            nc.sync.dma_start(out=ws_raw[0:P:8, w * H : (w + 1) * H].bitcast(I32), in_=rows[0].bitcast(I32))
+        nc.sync.dma_start(out=w2_raw[:, 2 * H :], in_=w2_rows[:, 2 * H :])
         nc.sync.dma_start(out=x_win[:, 0:X_HEAD].bitcast(I32), in_=words(x_words)[:, 0:X_HEAD])
         w1_head = tile("w1_head", P, I32)
         nc.sync.dma_start(out=w1_head[:], in_=words(w1_words)[:, 0:P])
@@ -94,8 +92,8 @@ def tile_picked_phlora_none_po_kernel(
         w2_plane = tile("w2_plane", H, U8)
         src = w2_raw[:].rearrange("p (j m t) -> p m j t", j=PACK, t=PACK)
         dst = w2_bf[:].rearrange("p (t m j) -> p m j t", j=PACK, t=PACK)
-        nc.scalar.copy(out=dst[:, 0:46], in_=src[:, 0:46])
-        nc.vector.tensor_copy(out=dst[:, 46:128], in_=src[:, 46:128])
+        nc.scalar.copy(out=dst[:, 0:64], in_=src[:, 0:64])
+        nc.vector.tensor_copy(out=dst[:, 64:128], in_=src[:, 64:128])
         nc.vector.quantize_mx(out=w2_codes[:].bitcast(FP8X4), scales=w2_plane[:], in_=w2_bf[:])
 
         x_all = tile("x_all", S, U32, tag="w2_then_x")
@@ -152,6 +150,7 @@ def tile_picked_phlora_none_po_kernel(
                 stop=False,
             )
 
+        y_rows = out_0.rearrange("(p t) c -> p t c", t=PACK)
         y = [tile("y%d" % a, PACK * HALF, F32) for a in range(2)]
 
         def second_term(a, t, copy):
@@ -165,13 +164,16 @@ def tile_picked_phlora_none_po_kernel(
                 stop=True,
             )
             copy(out=y[a][:, t * HALF : (t + 1) * HALF], in_=banks[a, t][:])
+            if t % 2 == 1:
+                nc.sync.dma_start(
+                    out=y_rows[:, t - 1 : t + 1, a * HALF : (a + 1) * HALF],
+                    in_=y[a][:, (t - 1) * HALF : (t + 1) * HALF].rearrange("p (t c) -> p t c", t=2),
+                )
 
-        y_rows = out_0.rearrange("(p t) c -> p t c", t=PACK)
         y_plane = tile("y_plane", S, U8)
 
         def hand_out(a, share):
             cols = slice(a * HALF, (a + 1) * HALF)
-            nc.sync.dma_start(out=y_rows[:, :, cols], in_=y[a][:].rearrange("p (t c) -> p t c", t=PACK))
             y_bf = tile("y_bf%d" % a, PACK * HALF, BF16)
             y_codes = tile("y_codes%d" % a, HALF, U32)
             dst = y_bf[:].rearrange("p (c i t) -> p c t i", i=4, t=PACK)

@@ -17,7 +17,11 @@ S = 512
 H = 512
 HALF = 256
 CHUNK = 128
-X_HEAD = 512
+LAST = 3
+Y_ON_SCALAR = (0, 0, 0, 16)
+W2_ON_SCALAR = (64, 40)
+WARM = 3
+SPLIT = (0, LAST)
 FLOPS = 3 * 2 * 512 * 512 * 512
 
 
@@ -31,6 +35,7 @@ def tile_picked_phlora_none_po_kernel(
 
     with ExitStack() as ctx:
         keep = ctx.enter_context(tc.tile_pool(name="keep", bufs=1))
+        shared = ctx.enter_context(tc.tile_pool(name="shared", bufs=1))
         psum = ctx.enter_context(tc.psum_pool(name="psum", bufs=1))
 
         def tile(name, cols, dtype, tag=None):
@@ -39,173 +44,234 @@ def tile_picked_phlora_none_po_kernel(
         offsets = keep.tile([P, S // 16], U16, name="offsets")
         xs_win = tile("xs_win", T, U8)
         ws_raw = tile("ws_raw", 2 * H, U8)
-        scales = tile("scales", S + 2 * H, U8)
+        all_scales = tile("all_scales", S + 2 * H, U8)
         x_win = tile("x_win", T, U32, tag="x_then_w")
-        w2_raw = tile("w2_raw", PACK * H, F32)
 
         nc.vector.memset(xs_win[:].bitcast(I32), 0)
-        nc.vector.memset(ws_raw[:].bitcast(I32), 0)
+        nc.gpsimd.memset(ws_raw[:].bitcast(I32), 0)
 
         seed = tile("seed", 16, F32)
         seed_bf = tile("seed_bf", 16, BF16)
         nc.gpsimd.memset(seed[:], 0.0)
         nc.scalar.copy(out=seed_bf[:], in_=seed[:])
 
+        w2_rows = w2.rearrange("(p j) c -> p j c", j=PACK)
+        w2_raw = [tile("w2_raw%d" % a, PACK * HALF, F32) for a in range(2)]
+
+        def load_w2(a, first, last):
+            nc.sync.dma_start(
+                out=w2_raw[a][:, first * HALF : last * HALF].rearrange("p (j c) -> p j c", c=HALF),
+                in_=w2_rows[:, first:last, a * HALF : (a + 1) * HALF],
+            )
+
+        load_w2(0, 0, 2)
         nc.sync.dma_start(offsets[:], offs)
-        w2_rows = w2.rearrange("(p j) c -> p (j c)", j=PACK)
-        nc.sync.dma_start(out=w2_raw[:, 0 : 2 * H], in_=w2_rows[:, 0 : 2 * H])
         nc.sync.dma_start(out=xs_win[0:P:8, :].bitcast(I32), in_=x_scales[0].bitcast(I32))
         for w, rows in enumerate((w1_scales, w3_scales)):
-            nc.sync.dma_start(out=ws_raw[0:P:8, w * H : (w + 1) * H].bitcast(I32), in_=rows[0].bitcast(I32))
-        nc.sync.dma_start(out=w2_raw[:, 2 * H :], in_=w2_rows[:, 2 * H :])
-        nc.sync.dma_start(out=x_win[:, 0:X_HEAD].bitcast(I32), in_=words(x_words)[:, 0:X_HEAD])
-        w1_head = tile("w1_head", P, I32)
-        nc.sync.dma_start(out=w1_head[:], in_=words(w1_words)[:, 0:P])
-        nc.sync.dma_start(out=x_win[:, X_HEAD:].bitcast(I32), in_=words(x_words)[:, X_HEAD:])
+            nc.scalar.dma_start(out=ws_raw[0:P:8, w * H : (w + 1) * H].bitcast(I32), in_=rows[0].bitcast(I32))
+        load_w2(0, 2, PACK)
+        load_w2(1, 0, PACK)
+        nc.sync.dma_start(out=x_win[:].bitcast(I32), in_=words(x_words))
+        w1_raw = tile("w1_raw", H, I32)
+        nc.sync.dma_start(out=w1_raw[:], in_=words(w1_words))
 
         xs_got = tile("xs_got", S, U8, tag="xs_then_w")
         nc.vector.tensor_copy(xs_got[:], xs_win[:].indirect(offsets[:]))
         nc.vector.tensor_copy(
-            out=scales[:, S:].rearrange("p (w t m) -> p w t m", w=2, t=PACK),
+            out=all_scales[:, S:].rearrange("p (w t m) -> p w t m", w=2, t=PACK),
             in_=ws_raw[:].rearrange("p (w m t) -> p w t m", w=2, t=PACK),
         )
-        nc.vector.tensor_copy(out=scales[:, 0:S].bitcast(I32), in_=xs_got[:].bitcast(I32))
+        nc.vector.tensor_copy(out=all_scales[:, 0:S].bitcast(I32), in_=xs_got[:].bitcast(I32))
         for j in range(1, PACK):
-            nc.sync.dma_start(out=scales[j:P:32, :].bitcast(I32), in_=scales[8 * j : P : 32, :].bitcast(I32))
-        warm = psum.tile([P, P], F32, name="warm", tag="early0")
-        for i in range(12):
+            nc.sync.dma_start(out=all_scales[j:P:32, :].bitcast(I32), in_=all_scales[8 * j : P : 32, :].bitcast(I32))
+        scales = all_scales[:, 0:S]
+        w1_plane = all_scales[:, S : S + H]
+        w3_plane = all_scales[:, S + H :]
+        w3_raw = tile("w3_raw", H, I32, tag="xs_then_w")
+        nc.sync.dma_start(out=w3_raw[:], in_=words(w3_words))
+
+        M_HALF = P // 2
+        w2_codes = tile("w2_codes", H, U32)
+        w2_plane = tile("w2_plane", H, U8)
+        w2_bf = [
+            shared.tile([P, PACK * HALF], BF16, name="w2_bf%d" % a, align_bytes=64, offset=2 * PACK * HALF * a)
+            for a in range(2)
+        ]
+        for a in range(2):
+            src = w2_raw[a][:].rearrange("p (j m t) -> p m j t", j=PACK, t=PACK)
+            dst = w2_bf[a][:].rearrange("p (t m j) -> p m j t", j=PACK, t=PACK)
+            share = W2_ON_SCALAR[a]
+            nc.scalar.copy(out=dst[:, :share], in_=src[:, :share])
+            if share < M_HALF:
+                nc.vector.tensor_copy(out=dst[:, share:], in_=src[:, share:])
+        for a in range(2):
+            for t in range(PACK):
+                cols = slice(t * P + a * M_HALF, t * P + (a + 1) * M_HALF)
+                nc.vector.quantize_mx(
+                    out=w2_codes[:, cols].bitcast(FP8X4),
+                    scales=w2_plane[:, cols],
+                    in_=w2_bf[a][:, t * HALF : (t + 1) * HALF],
+                )
+        warm = psum.tile([P, H], F32, name="warm", tag="y_acc0")
+        for i in range(WARM):
             nc.tensor.matmul_mx(
                 out=warm[:],
-                lhsT=w1_head[:].bitcast(FP8X4),
-                lhsT_scale=ws_raw[:, 0:P],
-                rhs=w1_head[:].bitcast(FP8X4),
-                rhs_scale=ws_raw[:, 0:P],
+                lhsT=w2_codes[:, 0:P].bitcast(FP8X4),
+                lhsT_scale=w2_plane[:, 0:P],
+                rhs=w2_codes[:].bitcast(FP8X4),
+                rhs_scale=w2_plane[:],
                 start=True,
                 stop=True,
             )
-        w_raw = tile("w_raw", 2 * H, I32, tag="xs_then_w")
-        nc.sync.dma_start(out=w_raw[:, P:H], in_=words(w1_words)[:, P:H])
-        nc.sync.dma_start(out=w_raw[:, H:], in_=words(w3_words))
 
-        w2_bf = tile("w2_bf", PACK * H, BF16, tag="w2_then_x")
-        w2_codes = tile("w2_codes", H, U32)
-        w2_plane = tile("w2_plane", H, U8)
-        src = w2_raw[:].rearrange("p (j m t) -> p m j t", j=PACK, t=PACK)
-        dst = w2_bf[:].rearrange("p (t m j) -> p m j t", j=PACK, t=PACK)
-        nc.scalar.copy(out=dst[:, 0:64], in_=src[:, 0:64])
-        nc.vector.tensor_copy(out=dst[:, 64:128], in_=src[:, 64:128])
-        nc.vector.quantize_mx(out=w2_codes[:].bitcast(FP8X4), scales=w2_plane[:], in_=w2_bf[:])
-
-        x_all = tile("x_all", S, U32, tag="w2_then_x")
-        x_got = [x_all[:, a * HALF : (a + 1) * HALF] for a in range(2)]
+        x_got = [
+            shared.tile([P, HALF], U32, name="x_got%d" % a, align_bytes=64, offset=2 * PACK * HALF + 4 * HALF * a)
+            for a in range(2)
+        ]
         for a in range(2):
-            nc.vector.tensor_copy(x_got[a], x_win[:].indirect(offsets[:, 16 * a : 16 * (a + 1)]))
+            nc.vector.tensor_copy(x_got[a][:], x_win[:].indirect(offsets[:, 16 * a : 16 * (a + 1)]))
+
+        def picked(c):
+            return x_got[c // 2][:, c % 2 * CHUNK : (c % 2 + 1) * CHUNK]
 
         w_dealt = tile("w_dealt", 2 * H, I32, tag="x_then_w")
+        w1_dealt = w_dealt[:, 0:H]
+        w3_dealt = w_dealt[:, H:]
 
-        def deal(w, source, first, count):
-            dealt = w_dealt[:, w * H : (w + 1) * H].rearrange("p (t m) -> p m t", t=PACK)
+        def deal(dealt, source):
             nc.vector.tensor_copy(
-                out=dealt[:, first // PACK : (first + count) // PACK, :],
+                out=dealt.rearrange("p (t m) -> p m t", t=PACK),
                 in_=source.rearrange("p (m t) -> p m t", t=PACK),
             )
 
-        h_bf = [tile("h_bf%d" % a, PACK * HALF, BF16) for a in range(2)]
-        h_codes = [tile("h_codes%d" % a, HALF, U32) for a in range(2)]
-        h_plane = [tile("h_plane%d" % a, HALF, U8) for a in range(2)]
+        deal(w1_dealt, w1_raw[:])
 
-        def hidden(chunk, copy):
-            bank = psum.tile([P, PACK * CHUNK], F32, name="h_acc%d" % chunk, tag="late%d" % chunk)
-            cols = slice(chunk * CHUNK, (chunk + 1) * CHUNK)
-            for t in range(PACK):
-                nc.tensor.matmul_mx(
-                    out=bank[:, t * CHUNK : (t + 1) * CHUNK],
-                    lhsT=w2_codes[:, t * P : (t + 1) * P].bitcast(FP8X4),
-                    lhsT_scale=w2_plane[:, t * P : (t + 1) * P],
-                    rhs=x_all[:, cols].bitcast(FP8X4),
-                    rhs_scale=scales[:, cols],
-                    start=True,
-                    stop=True,
-                )
-            c = chunk % 2
-            copy(
-                out=h_bf[chunk // 2][:, c * PACK * CHUNK : (c + 1) * PACK * CHUNK].rearrange("p (n t) -> p n t", t=PACK),
-                in_=bank[:].rearrange("p (t n) -> p n t", t=PACK),
-            )
-
-        def quantise_hidden(a):
-            nc.vector.quantize_mx(out=h_codes[a][:].bitcast(FP8X4), scales=h_plane[a][:], in_=h_bf[a][:])
-
-        banks = {}
-
-        def first_term(a, t):
-            banks[a, t] = psum.tile([P, HALF], F32, name="y_acc%d%d" % (a, t), tag=("early%d", "late%d")[a] % t)
-            nc.tensor.matmul_mx(
-                out=banks[a, t][:],
-                lhsT=w_dealt[:, t * P : (t + 1) * P].bitcast(FP8X4),
-                lhsT_scale=scales[:, S + t * P : S + (t + 1) * P],
-                rhs=x_got[a].bitcast(FP8X4),
-                rhs_scale=scales[:, a * HALF : (a + 1) * HALF],
-                start=True,
-                stop=False,
-            )
-
-        y_rows = out_0.rearrange("(p t) c -> p t c", t=PACK)
-        y = [tile("y%d" % a, PACK * HALF, F32) for a in range(2)]
-
-        def second_term(a, t, copy):
-            nc.tensor.matmul_mx(
-                out=banks[a, t][:],
-                lhsT=w_dealt[:, H + t * P : H + (t + 1) * P].bitcast(FP8X4),
-                lhsT_scale=scales[:, S + H + t * P : S + H + (t + 1) * P],
-                rhs=h_codes[a][:].bitcast(FP8X4),
-                rhs_scale=h_plane[a][:],
-                start=False,
-                stop=True,
-            )
-            copy(out=y[a][:, t * HALF : (t + 1) * HALF], in_=banks[a, t][:])
-            if t % 2 == 1:
-                nc.sync.dma_start(
-                    out=y_rows[:, t - 1 : t + 1, a * HALF : (a + 1) * HALF],
-                    in_=y[a][:, (t - 1) * HALF : (t + 1) * HALF].rearrange("p (t c) -> p t c", t=2),
-                )
-
+        chunks = range(S // CHUNK)
+        h_bf = [tile("h_bf%d" % c, PACK * CHUNK, BF16, tag="h_bf0" if c == 2 else None) for c in chunks]
+        h_codes = [tile("h_codes%d" % c, CHUNK, U32) for c in chunks]
+        h_plane = [tile("h_plane%d" % c, CHUNK, U8) for c in chunks]
+        y = [tile("y%d" % c, PACK * CHUNK, F32) for c in chunks]
+        y_bf = [tile("y_bf%d" % c, PACK * CHUNK, BF16) for c in chunks]
+        y_codes = tile("y_codes", S, U32)
         y_plane = tile("y_plane", S, U8)
+        y_rows = out_0.rearrange("(p t) c -> p t c", t=PACK)
+        h_acc = {}
+        y_acc = {}
 
-        def hand_out(a, share):
-            cols = slice(a * HALF, (a + 1) * HALF)
-            y_bf = tile("y_bf%d" % a, PACK * HALF, BF16)
-            y_codes = tile("y_codes%d" % a, HALF, U32)
-            dst = y_bf[:].rearrange("p (c i t) -> p c t i", i=4, t=PACK)
-            src = y[a][:].rearrange("p (t c i) -> p c t i", i=4, t=PACK)
+        def product(bank, t, w, w_scale, moving, moving_scale, start, stop):
+            nc.tensor.matmul_mx(
+                out=bank[:, t * CHUNK : (t + 1) * CHUNK],
+                lhsT=w[:, t * P : (t + 1) * P].bitcast(FP8X4),
+                lhsT_scale=w_scale[:, t * P : (t + 1) * P],
+                rhs=moving.bitcast(FP8X4),
+                rhs_scale=moving_scale,
+                start=start,
+                stop=stop,
+            )
+
+        def hidden(c):
+            cols = slice(c * CHUNK, (c + 1) * CHUNK)
+            h_acc[c] = psum.tile([P, PACK * CHUNK], F32, name="h_acc%d" % c, tag="h_acc%d" % c)
+            for t in range(PACK):
+                product(h_acc[c], t, w2_codes, w2_plane, picked(c), scales[:, cols], True, True)
+
+        def round_hidden(c, copy):
+            copy(
+                out=h_bf[c][:].rearrange("p (n t) -> p n t", t=PACK),
+                in_=h_acc[c][:].rearrange("p (t n) -> p n t", t=PACK),
+            )
+
+        def quantise_hidden(c):
+            nc.vector.quantize_mx(out=h_codes[c][:].bitcast(FP8X4), scales=h_plane[c][:], in_=h_bf[c][:])
+
+        def open_result(c):
+            bank = psum.tile([P, PACK * CHUNK], F32, name="y_acc%d" % c, tag=("y_acc0", "y_acc1", "h_acc1", "h_acc3")[c])
+            other = bank
+            if c in SPLIT:
+                other = psum.tile([P, PACK * CHUNK], F32, name="y_other%d" % c, tag="y_other0" if c == 0 else "h_acc2")
+            y_acc[c] = (bank, bank, other, other)
+
+        def term(c, w, w_plane, moving, moving_plane, first):
+            for t in range(PACK):
+                opens = first and (t == 0 or (c in SPLIT and t == 2))
+                closes = not first and (t == PACK - 1 or (c in SPLIT and t == 1))
+                product(y_acc[c][t], t, w, w_plane, moving, moving_plane, opens, closes)
+
+        def direct_term(c, first):
+            term(c, w1_dealt, w1_plane, picked(c), scales[:, c * CHUNK : (c + 1) * CHUNK], first)
+
+        def adapter_term(c, first):
+            term(c, w3_dealt, w3_plane, h_codes[c][:], h_plane[c][:], first)
+
+        def result(c):
+            open_result(c)
+            direct_term(c, True)
+            adapter_term(c, False)
+
+        def store(c, first, last):
+            nc.sync.dma_start(
+                out=y_rows[:, first:last, c * CHUNK : (c + 1) * CHUNK],
+                in_=y[c][:, first * CHUNK : last * CHUNK].rearrange("p (t n) -> p t n", n=CHUNK),
+            )
+
+        def store_result(c, copy):
+            if c == LAST:
+                nc.scalar.copy(out=y[c][:, :HALF], in_=y_acc[c][0][:, :HALF])
+                nc.scalar.copy(out=y[c][:, HALF:], in_=y_acc[c][2][:, HALF:])
+                store(c, 0, PACK)
+            elif c == 0:
+                copy(out=y[c][:, :HALF], in_=y_acc[c][0][:, :HALF])
+                store(c, 0, 2)
+                copy(out=y[c][:, HALF:], in_=y_acc[c][2][:, HALF:])
+                store(c, 2, PACK)
+            else:
+                copy(out=y[c][:], in_=y_acc[c][0][:])
+                store(c, 0, PACK)
+
+        def round_result(c):
+            dst = y_bf[c][:].rearrange("p (n i t) -> p n t i", i=4, t=PACK)
+            src = y[c][:].rearrange("p (t n i) -> p n t i", i=4, t=PACK)
+            share = Y_ON_SCALAR[c]
             if share:
                 nc.scalar.copy(out=dst[:, :share], in_=src[:, :share])
-            nc.vector.tensor_copy(out=dst[:, share:], in_=src[:, share:])
-            nc.vector.quantize_mx(out=y_codes[:].bitcast(FP8X4), scales=y_plane[:, cols], in_=y_bf[:])
-            nc.sync.dma_start(out=words(out_1)[:, cols], in_=y_codes[:].bitcast(I32))
+            if share < CHUNK // 4:
+                nc.vector.tensor_copy(out=dst[:, share:], in_=src[:, share:])
+
+        def quantise_result(c):
+            nc.vector.quantize_mx(
+                out=y_codes[:, c * CHUNK : (c + 1) * CHUNK].bitcast(FP8X4),
+                scales=y_plane[:, c * CHUNK : (c + 1) * CHUNK],
+                in_=y_bf[c][:],
+            )
+            if c % 2 == 1:
+                cols = slice((c - 1) * CHUNK, (c + 1) * CHUNK)
+                nc.sync.dma_start(out=words(out_1)[:, cols], in_=y_codes[:, cols].bitcast(I32))
 
         on_scalar = nc.scalar.copy
         on_vector = nc.vector.tensor_copy
-        hidden(0, on_scalar)
-        hidden(1, on_scalar)
-        deal(0, w1_head[:], 0, P)
-        deal(0, w_raw[:, P:H], P, H - P)
-        hidden(2, on_vector)
-        hidden(3, on_scalar)
-        deal(1, w_raw[:, H:], 0, H)
+        deal(w3_dealt, w3_raw[:])
+        for c in chunks:
+            hidden(c)
+        round_hidden(0, on_scalar)
+        round_hidden(1, on_scalar)
         quantise_hidden(0)
+        result(0)
+        round_hidden(2, on_vector)
         quantise_hidden(1)
-        for t in range(PACK):
-            first_term(0, t)
-        for t in range(PACK - 1):
-            first_term(1, t)
-        for t in range(PACK):
-            second_term(0, t, (on_scalar, on_vector)[t % 2])
-        first_term(1, PACK - 1)
-        hand_out(0, 0)
-        for t in range(PACK):
-            second_term(1, t, on_scalar)
-        hand_out(1, 24)
+        round_hidden(3, on_scalar)
+        result(1)
+        quantise_hidden(2)
+        store_result(0, on_scalar)
+        quantise_hidden(3)
+        for c in (2, 3):
+            result(c)
+        for c in chunks:
+            if c > 0:
+                store_result(c, on_scalar)
+            round_result(c)
+            if c > 0:
+                quantise_result(c - 1)
+        quantise_result(3)
         for q in range(4):
             queue = nc.sync if q % 2 == 0 else nc.scalar
             queue.dma_start(

@@ -64,12 +64,12 @@ def tile_picked_phlora_none_po_kernel(
                 in_=w2_rows[:, first:last, a * HALF : (a + 1) * HALF],
             )
 
-        load_w2(0, 0, 2)
+        load_w2(0, 0, 3)
         nc.sync.dma_start(offsets[:], offs)
         nc.sync.dma_start(out=xs_win[0:P:8, :].bitcast(I32), in_=x_scales[0].bitcast(I32))
         for w, rows in enumerate((w1_scales, w3_scales)):
-            nc.scalar.dma_start(out=ws_raw[0:P:8, w * H : (w + 1) * H].bitcast(I32), in_=rows[0].bitcast(I32))
-        load_w2(0, 2, PACK)
+            nc.sync.dma_start(out=ws_raw[0:P:8, w * H : (w + 1) * H].bitcast(I32), in_=rows[0].bitcast(I32))
+        load_w2(0, 3, PACK)
         load_w2(1, 0, PACK)
         nc.sync.dma_start(out=x_win[:].bitcast(I32), in_=words(x_words))
         w1_raw = tile("w1_raw", H, I32)

@@ -17,11 +17,17 @@ S = 512
 H = 512
 HALF = 256
 CHUNK = 128
-LAST = 3
-Y_ON_SCALAR = (0, 0, 0, 16)
-W2_ON_SCALAR = (64, 40)
-WARM = 3
-SPLIT = (0, LAST)
+CHUNKS = S // CHUNK
+LAST = CHUNKS - 1
+LIST_ROWS = 16
+QUADRANT = 32
+BLOCK_ROWS = 8
+
+W2_LEAD = 3
+W2_ON_SCALAR = 40
+Y_ON_SCALAR = 16
+WARM_PASSES = 3
+
 FLOPS = 3 * 2 * 512 * 512 * 512
 
 
@@ -41,7 +47,7 @@ def tile_picked_phlora_none_po_kernel(
         def tile(name, cols, dtype, tag=None):
             return keep.tile([P, cols], dtype, name=name, tag=tag or name, align_bytes=64)
 
-        offsets = keep.tile([P, S // 16], U16, name="offsets")
+        offsets = keep.tile([P, S // LIST_ROWS], U16, name="offsets")
         xs_win = tile("xs_win", T, U8)
         ws_raw = tile("ws_raw", 2 * H, U8)
         all_scales = tile("all_scales", S + 2 * H, U8)
@@ -64,12 +70,12 @@ def tile_picked_phlora_none_po_kernel(
                 in_=w2_rows[:, first:last, a * HALF : (a + 1) * HALF],
             )
 
-        load_w2(0, 0, 3)
+        load_w2(0, 0, W2_LEAD)
         nc.sync.dma_start(offsets[:], offs)
-        nc.sync.dma_start(out=xs_win[0:P:8, :].bitcast(I32), in_=x_scales[0].bitcast(I32))
+        nc.sync.dma_start(out=xs_win[0:P:BLOCK_ROWS, :].bitcast(I32), in_=x_scales[0].bitcast(I32))
         for w, rows in enumerate((w1_scales, w3_scales)):
-            nc.sync.dma_start(out=ws_raw[0:P:8, w * H : (w + 1) * H].bitcast(I32), in_=rows[0].bitcast(I32))
-        load_w2(0, 3, PACK)
+            nc.sync.dma_start(out=ws_raw[0:P:BLOCK_ROWS, w * H : (w + 1) * H].bitcast(I32), in_=rows[0].bitcast(I32))
+        load_w2(0, W2_LEAD, PACK)
         load_w2(1, 0, PACK)
         nc.sync.dma_start(out=x_win[:].bitcast(I32), in_=words(x_words))
         w1_raw = tile("w1_raw", H, I32)
@@ -83,37 +89,40 @@ def tile_picked_phlora_none_po_kernel(
         )
         nc.vector.tensor_copy(out=all_scales[:, 0:S].bitcast(I32), in_=xs_got[:].bitcast(I32))
         for j in range(1, PACK):
-            nc.sync.dma_start(out=all_scales[j:P:32, :].bitcast(I32), in_=all_scales[8 * j : P : 32, :].bitcast(I32))
-        scales = all_scales[:, 0:S]
+            nc.sync.dma_start(
+                out=all_scales[j:P:QUADRANT, :].bitcast(I32),
+                in_=all_scales[BLOCK_ROWS * j : P : QUADRANT, :].bitcast(I32),
+            )
+        x_plane = all_scales[:, 0:S]
         w1_plane = all_scales[:, S : S + H]
         w3_plane = all_scales[:, S + H :]
         w3_raw = tile("w3_raw", H, I32, tag="xs_then_w")
         nc.sync.dma_start(out=w3_raw[:], in_=words(w3_words))
 
-        M_HALF = P // 2
+        m_half = HALF // PACK
         w2_codes = tile("w2_codes", H, U32)
         w2_plane = tile("w2_plane", H, U8)
+        w2_bf_bytes = 2 * PACK * HALF
         w2_bf = [
-            shared.tile([P, PACK * HALF], BF16, name="w2_bf%d" % a, align_bytes=64, offset=2 * PACK * HALF * a)
+            shared.tile([P, PACK * HALF], BF16, name="w2_bf%d" % a, align_bytes=64, offset=w2_bf_bytes * a)
             for a in range(2)
         ]
-        for a in range(2):
-            src = w2_raw[a][:].rearrange("p (j m t) -> p m j t", j=PACK, t=PACK)
-            dst = w2_bf[a][:].rearrange("p (t m j) -> p m j t", j=PACK, t=PACK)
-            share = W2_ON_SCALAR[a]
-            nc.scalar.copy(out=dst[:, :share], in_=src[:, :share])
-            if share < M_HALF:
-                nc.vector.tensor_copy(out=dst[:, share:], in_=src[:, share:])
+        w2_src = [raw[:].rearrange("p (j m t) -> p m j t", j=PACK, t=PACK) for raw in w2_raw]
+        w2_dst = [bf[:].rearrange("p (t m j) -> p m j t", j=PACK, t=PACK) for bf in w2_bf]
+        nc.scalar.copy(out=w2_dst[0][:, :m_half], in_=w2_src[0][:, :m_half])
+        nc.scalar.copy(out=w2_dst[1][:, :W2_ON_SCALAR], in_=w2_src[1][:, :W2_ON_SCALAR])
+        nc.vector.tensor_copy(out=w2_dst[1][:, W2_ON_SCALAR:], in_=w2_src[1][:, W2_ON_SCALAR:])
         for a in range(2):
             for t in range(PACK):
-                cols = slice(t * P + a * M_HALF, t * P + (a + 1) * M_HALF)
+                cols = slice(t * P + a * m_half, t * P + (a + 1) * m_half)
                 nc.vector.quantize_mx(
                     out=w2_codes[:, cols].bitcast(FP8X4),
                     scales=w2_plane[:, cols],
                     in_=w2_bf[a][:, t * HALF : (t + 1) * HALF],
                 )
+
         warm = psum.tile([P, H], F32, name="warm", tag="y_acc0")
-        for i in range(WARM):
+        for i in range(WARM_PASSES):
             nc.tensor.matmul_mx(
                 out=warm[:],
                 lhsT=w2_codes[:, 0:P].bitcast(FP8X4),
@@ -125,14 +134,18 @@ def tile_picked_phlora_none_po_kernel(
             )
 
         x_got = [
-            shared.tile([P, HALF], U32, name="x_got%d" % a, align_bytes=64, offset=2 * PACK * HALF + 4 * HALF * a)
+            shared.tile([P, HALF], U32, name="x_got%d" % a, align_bytes=64, offset=w2_bf_bytes + 4 * HALF * a)
             for a in range(2)
         ]
+        list_cols = HALF // LIST_ROWS
         for a in range(2):
-            nc.vector.tensor_copy(x_got[a][:], x_win[:].indirect(offsets[:, 16 * a : 16 * (a + 1)]))
+            nc.vector.tensor_copy(x_got[a][:], x_win[:].indirect(offsets[:, list_cols * a : list_cols * (a + 1)]))
+
+        def places(c):
+            return slice(c * CHUNK, (c + 1) * CHUNK)
 
         def picked(c):
-            return x_got[c // 2][:, c % 2 * CHUNK : (c % 2 + 1) * CHUNK]
+            return x_got[c // 2][:, places(c % 2)]
 
         w_dealt = tile("w_dealt", 2 * H, I32, tag="x_then_w")
         w1_dealt = w_dealt[:, 0:H]
@@ -146,11 +159,11 @@ def tile_picked_phlora_none_po_kernel(
 
         deal(w1_dealt, w1_raw[:])
 
-        chunks = range(S // CHUNK)
-        h_bf = [tile("h_bf%d" % c, PACK * CHUNK, BF16, tag="h_bf0" if c == 2 else None) for c in chunks]
+        chunks = range(CHUNKS)
+        h_bf = [tile("h_bf%d" % c, PACK * CHUNK, BF16, tag="h_bf1" if c == LAST else None) for c in chunks]
         h_codes = [tile("h_codes%d" % c, CHUNK, U32) for c in chunks]
         h_plane = [tile("h_plane%d" % c, CHUNK, U8) for c in chunks]
-        y = [tile("y%d" % c, PACK * CHUNK, F32) for c in chunks]
+        y = [tile("y%d" % c, PACK * CHUNK, F32, tag="y_bf0" if c == LAST else None) for c in chunks]
         y_bf = [tile("y_bf%d" % c, PACK * CHUNK, BF16) for c in chunks]
         y_codes = tile("y_codes", S, U32)
         y_plane = tile("y_plane", S, U8)
@@ -158,22 +171,23 @@ def tile_picked_phlora_none_po_kernel(
         h_acc = {}
         y_acc = {}
 
-        def product(bank, t, w, w_scale, moving, moving_scale, start, stop):
+        y_banks = (("y_acc0", "y_other0"), ("y_acc1",), ("h_acc1",), ("h_acc2", "h_acc3"))
+
+        def product(bank, t, w, w_plane, moving, moving_plane, start, stop):
             nc.tensor.matmul_mx(
                 out=bank[:, t * CHUNK : (t + 1) * CHUNK],
                 lhsT=w[:, t * P : (t + 1) * P].bitcast(FP8X4),
-                lhsT_scale=w_scale[:, t * P : (t + 1) * P],
+                lhsT_scale=w_plane[:, t * P : (t + 1) * P],
                 rhs=moving.bitcast(FP8X4),
-                rhs_scale=moving_scale,
+                rhs_scale=moving_plane,
                 start=start,
                 stop=stop,
             )
 
         def hidden(c):
-            cols = slice(c * CHUNK, (c + 1) * CHUNK)
             h_acc[c] = psum.tile([P, PACK * CHUNK], F32, name="h_acc%d" % c, tag="h_acc%d" % c)
             for t in range(PACK):
-                product(h_acc[c], t, w2_codes, w2_plane, picked(c), scales[:, cols], True, True)
+                product(h_acc[c], t, w2_codes, w2_plane, picked(c), x_plane[:, places(c)], True, True)
 
         def round_hidden(c, copy):
             copy(
@@ -184,96 +198,80 @@ def tile_picked_phlora_none_po_kernel(
         def quantise_hidden(c):
             nc.vector.quantize_mx(out=h_codes[c][:].bitcast(FP8X4), scales=h_plane[c][:], in_=h_bf[c][:])
 
-        def open_result(c):
-            bank = psum.tile([P, PACK * CHUNK], F32, name="y_acc%d" % c, tag=("y_acc0", "y_acc1", "h_acc1", "h_acc3")[c])
-            other = bank
-            if c in SPLIT:
-                other = psum.tile([P, PACK * CHUNK], F32, name="y_other%d" % c, tag="y_other0" if c == 0 else "h_acc2")
-            y_acc[c] = (bank, bank, other, other)
-
-        def term(c, w, w_plane, moving, moving_plane, first):
-            for t in range(PACK):
-                opens = first and (t == 0 or (c in SPLIT and t == 2))
-                closes = not first and (t == PACK - 1 or (c in SPLIT and t == 1))
-                product(y_acc[c][t], t, w, w_plane, moving, moving_plane, opens, closes)
-
-        def direct_term(c, first):
-            term(c, w1_dealt, w1_plane, picked(c), scales[:, c * CHUNK : (c + 1) * CHUNK], first)
-
-        def adapter_term(c, first):
-            term(c, w3_dealt, w3_plane, h_codes[c][:], h_plane[c][:], first)
-
         def result(c):
-            open_result(c)
-            direct_term(c, True)
-            adapter_term(c, False)
+            y_acc[c] = [
+                psum.tile([P, PACK * CHUNK], F32, name="y_acc%d_%d" % (c, u), tag=tag)
+                for u, tag in enumerate(y_banks[c])
+            ]
+            per_bank = PACK // len(y_acc[c])
+            for t in range(PACK):
+                opens = t % per_bank == 0
+                product(y_acc[c][t // per_bank], t, w1_dealt, w1_plane, picked(c), x_plane[:, places(c)], opens, False)
+            for t in range(PACK):
+                closes = t % per_bank == per_bank - 1
+                product(y_acc[c][t // per_bank], t, w3_dealt, w3_plane, h_codes[c][:], h_plane[c][:], False, closes)
 
         def store(c, first, last):
             nc.sync.dma_start(
-                out=y_rows[:, first:last, c * CHUNK : (c + 1) * CHUNK],
+                out=y_rows[:, first:last, places(c)],
                 in_=y[c][:, first * CHUNK : last * CHUNK].rearrange("p (t n) -> p t n", n=CHUNK),
             )
 
-        def store_result(c, copy):
-            if c == LAST:
+        def store_result(c):
+            if c == 0:
                 nc.scalar.copy(out=y[c][:, :HALF], in_=y_acc[c][0][:, :HALF])
-                nc.scalar.copy(out=y[c][:, HALF:], in_=y_acc[c][2][:, HALF:])
+                store(c, 0, PACK // 2)
+                nc.scalar.copy(out=y[c][:, HALF:], in_=y_acc[c][1][:, HALF:])
+                store(c, PACK // 2, PACK)
+            elif c == LAST:
+                nc.scalar.copy(out=y[c][:, :HALF], in_=y_acc[c][0][:, :HALF])
+                nc.vector.tensor_copy(out=y[c][:, HALF:], in_=y_acc[c][1][:, HALF:])
                 store(c, 0, PACK)
-            elif c == 0:
-                copy(out=y[c][:, :HALF], in_=y_acc[c][0][:, :HALF])
-                store(c, 0, 2)
-                copy(out=y[c][:, HALF:], in_=y_acc[c][2][:, HALF:])
-                store(c, 2, PACK)
             else:
-                copy(out=y[c][:], in_=y_acc[c][0][:])
+                nc.scalar.copy(out=y[c][:], in_=y_acc[c][0][:])
                 store(c, 0, PACK)
 
         def round_result(c):
             dst = y_bf[c][:].rearrange("p (n i t) -> p n t i", i=4, t=PACK)
             src = y[c][:].rearrange("p (t n i) -> p n t i", i=4, t=PACK)
-            share = Y_ON_SCALAR[c]
+            share = Y_ON_SCALAR if c >= LAST - 1 else 0
             if share:
                 nc.scalar.copy(out=dst[:, :share], in_=src[:, :share])
-            if share < CHUNK // 4:
-                nc.vector.tensor_copy(out=dst[:, share:], in_=src[:, share:])
+            nc.vector.tensor_copy(out=dst[:, share:], in_=src[:, share:])
 
         def quantise_result(c):
             nc.vector.quantize_mx(
-                out=y_codes[:, c * CHUNK : (c + 1) * CHUNK].bitcast(FP8X4),
-                scales=y_plane[:, c * CHUNK : (c + 1) * CHUNK],
-                in_=y_bf[c][:],
+                out=y_codes[:, places(c)].bitcast(FP8X4), scales=y_plane[:, places(c)], in_=y_bf[c][:]
             )
             if c % 2 == 1:
-                cols = slice((c - 1) * CHUNK, (c + 1) * CHUNK)
-                nc.sync.dma_start(out=words(out_1)[:, cols], in_=y_codes[:, cols].bitcast(I32))
+                pair = slice((c - 1) * CHUNK, (c + 1) * CHUNK)
+                nc.sync.dma_start(out=words(out_1)[:, pair], in_=y_codes[:, pair].bitcast(I32))
 
-        on_scalar = nc.scalar.copy
-        on_vector = nc.vector.tensor_copy
         deal(w3_dealt, w3_raw[:])
         for c in chunks:
             hidden(c)
-        round_hidden(0, on_scalar)
-        round_hidden(1, on_scalar)
+        round_hidden(0, nc.scalar.copy)
+        round_hidden(1, nc.scalar.copy)
         quantise_hidden(0)
         result(0)
-        round_hidden(2, on_vector)
+        round_hidden(2, nc.scalar.copy)
         quantise_hidden(1)
-        round_hidden(3, on_scalar)
+        round_hidden(3, nc.vector.tensor_copy)
         result(1)
         quantise_hidden(2)
-        store_result(0, on_scalar)
+        store_result(0)
         quantise_hidden(3)
-        for c in (2, 3):
-            result(c)
-        for c in chunks:
-            if c > 0:
-                store_result(c, on_scalar)
+        result(2)
+        result(3)
+        round_result(0)
+        for c in range(1, CHUNKS):
+            store_result(c)
             round_result(c)
-            if c > 0:
-                quantise_result(c - 1)
-        quantise_result(3)
-        for q in range(4):
-            queue = nc.sync if q % 2 == 0 else nc.scalar
+            quantise_result(c - 1)
+        quantise_result(LAST)
+        for g in range(P // QUADRANT):
+            queue = nc.sync if g % 2 == 0 else nc.scalar
             queue.dma_start(
-                out=out_2[0][4 * q : 4 * q + 4, :].bitcast(I32), in_=y_plane[32 * q : 32 * q + 4, :].bitcast(I32)
+                out=out_2[0][PACK * g : PACK * (g + 1), :].bitcast(I32),
+                in_=y_plane[QUADRANT * g : QUADRANT * g + PACK, :].bitcast(I32),
             )

@@ -243,9 +243,6 @@ def tile_picked_phlora_none_po_kernel(
             nc.vector.quantize_mx(
                 out=y_codes[:, places(c)].bitcast(FP8X4), scales=y_plane[:, places(c)], in_=y_bf[c][:]
             )
-            if c % 2 == 1:
-                pair = slice((c - 1) * CHUNK, (c + 1) * CHUNK)
-                nc.sync.dma_start(out=words(out_1)[:, pair], in_=y_codes[:, pair].bitcast(I32))
 
         deal(w3_dealt, w3_raw[:])
         for c in chunks:
@@ -269,6 +266,7 @@ def tile_picked_phlora_none_po_kernel(
             round_result(c)
             quantise_result(c - 1)
         quantise_result(LAST)
+        nc.sync.dma_start(out=words(out_1), in_=y_codes[:].bitcast(I32))
         for g in range(P // QUADRANT):
             queue = nc.sync if g % 2 == 0 else nc.scalar
             queue.dma_start(

@@ -160,7 +160,7 @@ def tile_picked_phlora_none_po_kernel(
         deal(w1_dealt, w1_raw[:])
 
         chunks = range(CHUNKS)
-        h_bf = [tile("h_bf%d" % c, PACK * CHUNK, BF16, tag="h_bf1" if c == LAST else None) for c in chunks]
+        h_bf = [tile("h_bf%d" % c, PACK * CHUNK, BF16, tag=None) for c in chunks]
         h_codes = [tile("h_codes%d" % c, CHUNK, U32) for c in chunks]
         h_plane = [tile("h_plane%d" % c, CHUNK, U8) for c in chunks]
         y = [tile("y%d" % c, PACK * CHUNK, F32, tag="y_bf0" if c == LAST else None) for c in chunks]
@@ -171,7 +171,7 @@ def tile_picked_phlora_none_po_kernel(
         h_acc = {}
         y_acc = {}
 
-        y_banks = (("y_acc0", "y_other0"), ("y_acc1",), ("h_acc1",), ("h_acc2", "h_acc3"))
+        y_banks = (("y_acc0", "y_other0"), ("y_acc1",), ("h_acc2",), ("h_acc3", "h_acc1"))
 
         def product(bank, t, w, w_plane, moving, moving_plane, start, stop):
             nc.tensor.matmul_mx(
@@ -248,12 +248,12 @@ def tile_picked_phlora_none_po_kernel(
         for c in chunks:
             hidden(c)
         round_hidden(0, nc.scalar.copy)
-        round_hidden(1, nc.scalar.copy)
+        round_hidden(1, nc.vector.tensor_copy)
         quantise_hidden(0)
         result(0)
         round_hidden(2, nc.scalar.copy)
         quantise_hidden(1)
-        round_hidden(3, nc.vector.tensor_copy)
+        round_hidden(3, nc.scalar.copy)
         result(1)
         quantise_hidden(2)
         store_result(0)

@@ -24,7 +24,7 @@ QUADRANT = 32
 BLOCK_ROWS = 8
 
 W2_LEAD = 3
-W2_ON_SCALAR = 40
+W2_ON_SCALAR = 36
 Y_ON_SCALAR = 16
 WARM_PASSES = 3
 
@@ -72,9 +72,9 @@ def tile_picked_phlora_none_po_kernel(
 
         load_w2(0, 0, W2_LEAD)
         nc.sync.dma_start(offsets[:], offs)
-        nc.sync.dma_start(out=xs_win[0:P:BLOCK_ROWS, :].bitcast(I32), in_=x_scales[0].bitcast(I32))
         for w, rows in enumerate((w1_scales, w3_scales)):
             nc.sync.dma_start(out=ws_raw[0:P:BLOCK_ROWS, w * H : (w + 1) * H].bitcast(I32), in_=rows[0].bitcast(I32))
+        nc.sync.dma_start(out=xs_win[0:P:BLOCK_ROWS, :].bitcast(I32), in_=x_scales[0].bitcast(I32))
         load_w2(0, W2_LEAD, PACK)
         load_w2(1, 0, PACK)
         nc.sync.dma_start(out=x_win[:].bitcast(I32), in_=words(x_words))
@@ -82,11 +82,11 @@ def tile_picked_phlora_none_po_kernel(
         nc.sync.dma_start(out=w1_raw[:], in_=words(w1_words))
 
         xs_got = tile("xs_got", S, U8, tag="xs_then_w")
-        nc.vector.tensor_copy(xs_got[:], xs_win[:].indirect(offsets[:]))
         nc.vector.tensor_copy(
             out=all_scales[:, S:].rearrange("p (w t m) -> p w t m", w=2, t=PACK),
             in_=ws_raw[:].rearrange("p (w m t) -> p w t m", w=2, t=PACK),
         )
+        nc.vector.tensor_copy(xs_got[:], xs_win[:].indirect(offsets[:]))
         nc.vector.tensor_copy(out=all_scales[:, 0:S].bitcast(I32), in_=xs_got[:].bitcast(I32))
         for j in range(1, PACK):
             nc.sync.dma_start(

@@ -78,8 +78,8 @@ def tile_picked_phlora_none_po_kernel(
         load_w2(0, W2_LEAD, PACK)
         load_w2(1, 0, PACK)
         nc.sync.dma_start(out=x_win[:].bitcast(I32), in_=words(x_words))
-        w1_raw = tile("w1_raw", H, I32)
-        nc.sync.dma_start(out=w1_raw[:], in_=words(w1_words))
+        w1_raw = tile("w1_raw", H, U32)
+        nc.sync.dma_start(out=w1_raw[:].bitcast(I32), in_=words(w1_words))
 
         xs_got = tile("xs_got", S, U8, tag="xs_then_w")
         nc.vector.tensor_copy(
@@ -157,7 +157,12 @@ def tile_picked_phlora_none_po_kernel(
                 in_=source.rearrange("p (m t) -> p m t", t=PACK),
             )
 
-        deal(w1_dealt, w1_raw[:])
+        w1_tile = tile("w1_dealt", H, U32)
+        w1_dealt = w1_tile[:]
+        nc.scalar.copy(
+            out=w1_dealt.rearrange("p (t m) -> p m t", t=PACK),
+            in_=w1_raw[:].rearrange("p (m t) -> p m t", t=PACK),
+        )
 
         chunks = range(CHUNKS)
         h_bf = [tile("h_bf%d" % c, PACK * CHUNK, BF16, tag=None) for c in chunks]
@@ -171,7 +176,7 @@ def tile_picked_phlora_none_po_kernel(
         h_acc = {}
         y_acc = {}
 
-        y_banks = (("y_acc0", "y_other0"), ("y_acc1",), ("h_acc2",), ("h_acc3", "h_acc1"))
+        y_banks = (("y_acc0", "y_other0"), ("y_acc1", "y_other1"), ("h_acc2",), ("h_acc3", "h_acc1"))
 
         def product(bank, t, w, w_plane, moving, moving_plane, start, stop):
             nc.tensor.matmul_mx(
@@ -223,7 +228,7 @@ def tile_picked_phlora_none_po_kernel(
                 store(c, 0, PACK // 2)
                 nc.scalar.copy(out=y[c][:, HALF:], in_=y_acc[c][1][:, HALF:])
                 store(c, PACK // 2, PACK)
-            elif c == LAST:
+            elif c in (1, LAST):
                 nc.scalar.copy(out=y[c][:, :HALF], in_=y_acc[c][0][:, :HALF])
                 nc.vector.tensor_copy(out=y[c][:, HALF:], in_=y_acc[c][1][:, HALF:])
                 store(c, 0, PACK)
@@ -265,8 +270,10 @@ def tile_picked_phlora_none_po_kernel(
             store_result(c)
             round_result(c)
             quantise_result(c - 1)
+            if c == 2:
+                nc.sync.dma_start(out=words(out_1)[:, :HALF], in_=y_codes[:, :HALF].bitcast(I32))
         quantise_result(LAST)
-        nc.sync.dma_start(out=words(out_1), in_=y_codes[:].bitcast(I32))
+        nc.sync.dma_start(out=words(out_1)[:, HALF:], in_=y_codes[:, HALF:].bitcast(I32))
         for g in range(P // QUADRANT):
             queue = nc.sync if g % 2 == 0 else nc.scalar
             queue.dma_start(

@@ -24,9 +24,9 @@ QUADRANT = 32
 BLOCK_ROWS = 8
 
 W2_LEAD = 3
-W2_ON_SCALAR = 36
-Y_ON_SCALAR = 16
-WARM_PASSES = 3
+W2_ON_SCALAR = 24
+Y_ON_SCALAR = (0, 0, 20, 14)
+WARM_WIDTHS = (256, 256, 512, 512)
 
 FLOPS = 3 * 2 * 512 * 512 * 512
 
@@ -50,7 +50,8 @@ def tile_picked_phlora_none_po_kernel(
         offsets = keep.tile([P, S // LIST_ROWS], U16, name="offsets")
         xs_win = tile("xs_win", T, U8)
         ws_raw = tile("ws_raw", 2 * H, U8)
-        all_scales = tile("all_scales", S + 2 * H, U8)
+        x_plane = tile("x_plane", S, U8)
+        w_planes = shared.tile([P, 2 * H], U8, name="w_planes", align_bytes=64, offset=0)
         x_win = tile("x_win", T, U32, tag="x_then_w")
 
         nc.vector.memset(xs_win[:].bitcast(I32), 0)
@@ -72,32 +73,31 @@ def tile_picked_phlora_none_po_kernel(
 
         load_w2(0, 0, W2_LEAD)
         nc.sync.dma_start(offsets[:], offs)
+        nc.sync.dma_start(out=xs_win[0:P:BLOCK_ROWS, :].bitcast(I32), in_=x_scales[0].bitcast(I32))
         for w, rows in enumerate((w1_scales, w3_scales)):
             nc.sync.dma_start(out=ws_raw[0:P:BLOCK_ROWS, w * H : (w + 1) * H].bitcast(I32), in_=rows[0].bitcast(I32))
-        nc.sync.dma_start(out=xs_win[0:P:BLOCK_ROWS, :].bitcast(I32), in_=x_scales[0].bitcast(I32))
         load_w2(0, W2_LEAD, PACK)
         load_w2(1, 0, PACK)
         nc.sync.dma_start(out=x_win[:].bitcast(I32), in_=words(x_words))
-        w1_raw = tile("w1_raw", H, U32)
-        nc.sync.dma_start(out=w1_raw[:].bitcast(I32), in_=words(w1_words))
+        w1_words_raw = tile("w1_raw", H, U32)
+        w1_raw = w1_words_raw[:]
+        nc.sync.dma_start(out=w1_raw.bitcast(I32), in_=words(w1_words))
 
         xs_got = tile("xs_got", S, U8, tag="xs_then_w")
-        nc.vector.tensor_copy(
-            out=all_scales[:, S:].rearrange("p (w t m) -> p w t m", w=2, t=PACK),
-            in_=ws_raw[:].rearrange("p (w m t) -> p w t m", w=2, t=PACK),
-        )
+
+        def place_rows(plane):
+            for j in range(1, PACK):
+                nc.sync.dma_start(
+                    out=plane[j:P:QUADRANT, :].bitcast(I32),
+                    in_=plane[BLOCK_ROWS * j : P : QUADRANT, :].bitcast(I32),
+                )
+
         nc.vector.tensor_copy(xs_got[:], xs_win[:].indirect(offsets[:]))
-        nc.vector.tensor_copy(out=all_scales[:, 0:S].bitcast(I32), in_=xs_got[:].bitcast(I32))
-        for j in range(1, PACK):
-            nc.sync.dma_start(
-                out=all_scales[j:P:QUADRANT, :].bitcast(I32),
-                in_=all_scales[BLOCK_ROWS * j : P : QUADRANT, :].bitcast(I32),
-            )
-        x_plane = all_scales[:, 0:S]
-        w1_plane = all_scales[:, S : S + H]
-        w3_plane = all_scales[:, S + H :]
-        w3_raw = tile("w3_raw", H, I32, tag="xs_then_w")
-        nc.sync.dma_start(out=w3_raw[:], in_=words(w3_words))
+        nc.vector.tensor_copy(out=x_plane[:].bitcast(I32), in_=xs_got[:].bitcast(I32))
+        place_rows(x_plane)
+        w3_words_raw = tile("w3_raw", H, I32, tag="xs_then_w")
+        w3_raw = w3_words_raw[:]
+        nc.sync.dma_start(out=w3_raw, in_=words(w3_words))
 
         m_half = HALF // PACK
         w2_codes = tile("w2_codes", H, U32)
@@ -121,14 +121,22 @@ def tile_picked_phlora_none_po_kernel(
                     in_=w2_bf[a][:, t * HALF : (t + 1) * HALF],
                 )
 
+        nc.vector.tensor_copy(
+            out=w_planes[:].rearrange("p (w t m) -> p w t m", w=2, t=PACK),
+            in_=ws_raw[:].rearrange("p (w m t) -> p w t m", w=2, t=PACK),
+        )
+        place_rows(w_planes)
+        w1_plane = w_planes[:, 0:H]
+        w3_plane = w_planes[:, H:]
+
         warm = psum.tile([P, H], F32, name="warm", tag="y_acc0")
-        for i in range(WARM_PASSES):
+        for width in WARM_WIDTHS:
             nc.tensor.matmul_mx(
-                out=warm[:],
+                out=warm[:, :width],
                 lhsT=w2_codes[:, 0:P].bitcast(FP8X4),
                 lhsT_scale=w2_plane[:, 0:P],
-                rhs=w2_codes[:].bitcast(FP8X4),
-                rhs_scale=w2_plane[:],
+                rhs=w2_codes[:, :width].bitcast(FP8X4),
+                rhs_scale=w2_plane[:, :width],
                 start=True,
                 stop=True,
             )
@@ -140,6 +148,7 @@ def tile_picked_phlora_none_po_kernel(
         list_cols = HALF // LIST_ROWS
         for a in range(2):
             nc.vector.tensor_copy(x_got[a][:], x_win[:].indirect(offsets[:, list_cols * a : list_cols * (a + 1)]))
+
 
         def places(c):
             return slice(c * CHUNK, (c + 1) * CHUNK)
@@ -161,14 +170,18 @@ def tile_picked_phlora_none_po_kernel(
         w1_dealt = w1_tile[:]
         nc.scalar.copy(
             out=w1_dealt.rearrange("p (t m) -> p m t", t=PACK),
-            in_=w1_raw[:].rearrange("p (m t) -> p m t", t=PACK),
+            in_=w1_raw.rearrange("p (m t) -> p m t", t=PACK),
         )
 
         chunks = range(CHUNKS)
         h_bf = [tile("h_bf%d" % c, PACK * CHUNK, BF16, tag=None) for c in chunks]
         h_codes = [tile("h_codes%d" % c, CHUNK, U32) for c in chunks]
         h_plane = [tile("h_plane%d" % c, CHUNK, U8) for c in chunks]
-        y = [tile("y%d" % c, PACK * CHUNK, F32, tag="y_bf0" if c == LAST else None) for c in chunks]
+        y_first = [tile("y%d" % c, PACK * CHUNK, F32) for c in range(2)]
+        y_last = tile("y_last", PACK * HALF, F32)
+        y = [t[:].rearrange("p (t n) -> p t n", t=PACK) for t in y_first]
+        y_pair = y_last[:].rearrange("p (t n) -> p t n", t=PACK)
+        y = y + [y_pair[:, :, places(c)] for c in range(2)]
         y_bf = [tile("y_bf%d" % c, PACK * CHUNK, BF16) for c in chunks]
         y_codes = tile("y_codes", S, U32)
         y_plane = tile("y_plane", S, U8)
@@ -203,7 +216,7 @@ def tile_picked_phlora_none_po_kernel(
         def quantise_hidden(c):
             nc.vector.quantize_mx(out=h_codes[c][:].bitcast(FP8X4), scales=h_plane[c][:], in_=h_bf[c][:])
 
-        def result(c):
+        def direct(c):
             y_acc[c] = [
                 psum.tile([P, PACK * CHUNK], F32, name="y_acc%d_%d" % (c, u), tag=tag)
                 for u, tag in enumerate(y_banks[c])
@@ -212,34 +225,41 @@ def tile_picked_phlora_none_po_kernel(
             for t in range(PACK):
                 opens = t % per_bank == 0
                 product(y_acc[c][t // per_bank], t, w1_dealt, w1_plane, picked(c), x_plane[:, places(c)], opens, False)
+
+        def adapter(c):
+            per_bank = PACK // len(y_acc[c])
             for t in range(PACK):
                 closes = t % per_bank == per_bank - 1
                 product(y_acc[c][t // per_bank], t, w3_dealt, w3_plane, h_codes[c][:], h_plane[c][:], False, closes)
 
         def store(c, first, last):
-            nc.sync.dma_start(
-                out=y_rows[:, first:last, places(c)],
-                in_=y[c][:, first * CHUNK : last * CHUNK].rearrange("p (t n) -> p t n", n=CHUNK),
-            )
+            nc.sync.dma_start(out=y_rows[:, first:last, places(c)], in_=y[c][:, first:last])
+
+        def empty(c, u, copy):
+            per_bank = PACK // len(y_acc[c])
+            rows = slice(u * per_bank, (u + 1) * per_bank)
+            copy(out=y[c][:, rows], in_=y_acc[c][u][:].rearrange("p (t n) -> p t n", t=PACK)[:, rows])
 
         def store_result(c):
             if c == 0:
-                nc.scalar.copy(out=y[c][:, :HALF], in_=y_acc[c][0][:, :HALF])
+                empty(c, 0, nc.scalar.copy)
                 store(c, 0, PACK // 2)
-                nc.scalar.copy(out=y[c][:, HALF:], in_=y_acc[c][1][:, HALF:])
+                empty(c, 1, nc.scalar.copy)
                 store(c, PACK // 2, PACK)
-            elif c in (1, LAST):
-                nc.scalar.copy(out=y[c][:, :HALF], in_=y_acc[c][0][:, :HALF])
-                nc.vector.tensor_copy(out=y[c][:, HALF:], in_=y_acc[c][1][:, HALF:])
-                store(c, 0, PACK)
+            elif c == 2:
+                empty(c, 0, nc.scalar.copy)
             else:
-                nc.scalar.copy(out=y[c][:], in_=y_acc[c][0][:])
-                store(c, 0, PACK)
+                empty(c, 0, nc.scalar.copy)
+                empty(c, 1, nc.vector.tensor_copy)
+                if c == LAST:
+                    nc.sync.dma_start(out=y_rows[:, :, HALF:], in_=y_pair)
+                else:
+                    store(c, 0, PACK)
 
         def round_result(c):
             dst = y_bf[c][:].rearrange("p (n i t) -> p n t i", i=4, t=PACK)
-            src = y[c][:].rearrange("p (t n i) -> p n t i", i=4, t=PACK)
-            share = Y_ON_SCALAR if c >= LAST - 1 else 0
+            src = y[c].rearrange("p t (n i) -> p n t i", i=4)
+            share = Y_ON_SCALAR[c]
             if share:
                 nc.scalar.copy(out=dst[:, :share], in_=src[:, :share])
             nc.vector.tensor_copy(out=dst[:, share:], in_=src[:, share:])
@@ -249,30 +269,39 @@ def tile_picked_phlora_none_po_kernel(
                 out=y_codes[:, places(c)].bitcast(FP8X4), scales=y_plane[:, places(c)], in_=y_bf[c][:]
             )
 
-        deal(w3_dealt, w3_raw[:])
+        deal(w3_dealt, w3_raw)
         for c in chunks:
             hidden(c)
+        direct(0)
+        direct(1)
         round_hidden(0, nc.scalar.copy)
         round_hidden(1, nc.vector.tensor_copy)
         quantise_hidden(0)
-        result(0)
+        adapter(0)
         round_hidden(2, nc.scalar.copy)
         quantise_hidden(1)
         round_hidden(3, nc.scalar.copy)
-        result(1)
+        adapter(1)
         quantise_hidden(2)
         store_result(0)
         quantise_hidden(3)
-        result(2)
-        result(3)
+        direct(2)
+        adapter(2)
+        direct(3)
+        adapter(3)
+
+        store_result(1)
         round_result(0)
-        for c in range(1, CHUNKS):
-            store_result(c)
-            round_result(c)
-            quantise_result(c - 1)
-            if c == 2:
-                nc.sync.dma_start(out=words(out_1)[:, :HALF], in_=y_codes[:, :HALF].bitcast(I32))
-        quantise_result(LAST)
+        round_result(1)
+        quantise_result(0)
+        store_result(2)
+        store_result(3)
+        quantise_result(1)
+        nc.sync.dma_start(out=words(out_1)[:, :HALF], in_=y_codes[:, :HALF].bitcast(I32))
+        round_result(2)
+        round_result(3)
+        quantise_result(2)
+        quantise_result(3)
         nc.sync.dma_start(out=words(out_1)[:, HALF:], in_=y_codes[:, HALF:].bitcast(I32))
         for g in range(P // QUADRANT):
             queue = nc.sync if g % 2 == 0 else nc.scalar

@@ -25,7 +25,7 @@ BLOCK_ROWS = 8
 
 W2_LEAD = 3
 W2_ON_SCALAR = 24
-Y_ON_SCALAR = (0, 0, 20, 14)
+Y_ON_SCALAR = (0, 0, 0, 32)
 WARM_WIDTHS = (256, 256, 512, 512)
 
 FLOPS = 3 * 2 * 512 * 512 * 512
@@ -112,14 +112,15 @@ def tile_picked_phlora_none_po_kernel(
         nc.scalar.copy(out=w2_dst[0][:, :m_half], in_=w2_src[0][:, :m_half])
         nc.scalar.copy(out=w2_dst[1][:, :W2_ON_SCALAR], in_=w2_src[1][:, :W2_ON_SCALAR])
         nc.vector.tensor_copy(out=w2_dst[1][:, W2_ON_SCALAR:], in_=w2_src[1][:, W2_ON_SCALAR:])
-        for a in range(2):
-            for t in range(PACK):
-                cols = slice(t * P + a * m_half, t * P + (a + 1) * m_half)
-                nc.vector.quantize_mx(
-                    out=w2_codes[:, cols].bitcast(FP8X4),
-                    scales=w2_plane[:, cols],
-                    in_=w2_bf[a][:, t * HALF : (t + 1) * HALF],
-                )
+        for pair in range(2):
+            for a in range(2):
+                for t in (2 * pair, 2 * pair + 1):
+                    cols = slice(t * P + a * m_half, t * P + (a + 1) * m_half)
+                    nc.vector.quantize_mx(
+                        out=w2_codes[:, cols].bitcast(FP8X4),
+                        scales=w2_plane[:, cols],
+                        in_=w2_bf[a][:, t * HALF : (t + 1) * HALF],
+                    )
 
         nc.vector.tensor_copy(
             out=w_planes[:].rearrange("p (w t m) -> p w t m", w=2, t=PACK),
@@ -174,15 +175,14 @@ def tile_picked_phlora_none_po_kernel(
         )
 
         chunks = range(CHUNKS)
-        h_bf = [tile("h_bf%d" % c, PACK * CHUNK, BF16, tag=None) for c in chunks]
+        h_bf = [tile("h_bf%d" % c, PACK * CHUNK, BF16, tag="h_bf1" if c == LAST else None) for c in chunks]
         h_codes = [tile("h_codes%d" % c, CHUNK, U32) for c in chunks]
         h_plane = [tile("h_plane%d" % c, CHUNK, U8) for c in chunks]
-        y_first = [tile("y%d" % c, PACK * CHUNK, F32) for c in range(2)]
-        y_last = tile("y_last", PACK * HALF, F32)
-        y = [t[:].rearrange("p (t n) -> p t n", t=PACK) for t in y_first]
-        y_pair = y_last[:].rearrange("p (t n) -> p t n", t=PACK)
-        y = y + [y_pair[:, :, places(c)] for c in range(2)]
-        y_bf = [tile("y_bf%d" % c, PACK * CHUNK, BF16) for c in chunks]
+        y_tiles = [tile("y%d" % g, PACK * HALF, F32) for g in range(2)]
+        y_half = [y_tile[:].rearrange("p (t n) -> p t n", t=PACK) for y_tile in y_tiles]
+        y = [y_half[c // 2][:, :, places(c % 2)] for c in chunks]
+        y_bf_half = [tile("y_bf%d" % g, PACK * HALF, BF16) for g in range(2)]
+        y_bf = [y_bf_half[c // 2][:, (c % 2) * H : (c % 2 + 1) * H] for c in chunks]
         y_codes = tile("y_codes", S, U32)
         y_plane = tile("y_plane", S, U8)
         y_rows = out_0.rearrange("(p t) c -> p t c", t=PACK)
@@ -232,42 +232,31 @@ def tile_picked_phlora_none_po_kernel(
                 closes = t % per_bank == per_bank - 1
                 product(y_acc[c][t // per_bank], t, w3_dealt, w3_plane, h_codes[c][:], h_plane[c][:], False, closes)
 
-        def store(c, first, last):
-            nc.sync.dma_start(out=y_rows[:, first:last, places(c)], in_=y[c][:, first:last])
+        def store(first, last, cols):
+            g = cols.start // HALF
+            nc.sync.dma_start(
+                out=y_rows[:, first:last, cols],
+                in_=y_half[g][:, first:last, cols.start - g * HALF : cols.stop - g * HALF],
+            )
 
         def empty(c, u, copy):
             per_bank = PACK // len(y_acc[c])
             rows = slice(u * per_bank, (u + 1) * per_bank)
             copy(out=y[c][:, rows], in_=y_acc[c][u][:].rearrange("p (t n) -> p t n", t=PACK)[:, rows])
 
-        def store_result(c):
-            if c == 0:
-                empty(c, 0, nc.scalar.copy)
-                store(c, 0, PACK // 2)
-                empty(c, 1, nc.scalar.copy)
-                store(c, PACK // 2, PACK)
-            elif c == 2:
-                empty(c, 0, nc.scalar.copy)
-            else:
-                empty(c, 0, nc.scalar.copy)
-                empty(c, 1, nc.vector.tensor_copy)
-                if c == LAST:
-                    nc.sync.dma_start(out=y_rows[:, :, HALF:], in_=y_pair)
-                else:
-                    store(c, 0, PACK)
-
         def round_result(c):
-            dst = y_bf[c][:].rearrange("p (n i t) -> p n t i", i=4, t=PACK)
+            dst = y_bf[c].rearrange("p (n i t) -> p n t i", i=4, t=PACK)
             src = y[c].rearrange("p t (n i) -> p n t i", i=4)
             share = Y_ON_SCALAR[c]
             if share:
                 nc.scalar.copy(out=dst[:, :share], in_=src[:, :share])
-            nc.vector.tensor_copy(out=dst[:, share:], in_=src[:, share:])
+            if share < CHUNK // 4:
+                nc.vector.tensor_copy(out=dst[:, share:], in_=src[:, share:])
 
-        def quantise_result(c):
-            nc.vector.quantize_mx(
-                out=y_codes[:, places(c)].bitcast(FP8X4), scales=y_plane[:, places(c)], in_=y_bf[c][:]
-            )
+        def quantise_result(first, last):
+            cols = slice(first * CHUNK, last * CHUNK)
+            rounded = y_bf_half[first // 2][:, (first % 2) * H : ((last - 1) % 2 + 1) * H]
+            nc.vector.quantize_mx(out=y_codes[:, cols].bitcast(FP8X4), scales=y_plane[:, cols], in_=rounded)
 
         deal(w3_dealt, w3_raw)
         for c in chunks:
@@ -280,29 +269,35 @@ def tile_picked_phlora_none_po_kernel(
         adapter(0)
         round_hidden(2, nc.scalar.copy)
         quantise_hidden(1)
-        round_hidden(3, nc.scalar.copy)
         adapter(1)
+        round_hidden(3, nc.vector.tensor_copy)
         quantise_hidden(2)
-        store_result(0)
         quantise_hidden(3)
         direct(2)
         adapter(2)
         direct(3)
         adapter(3)
-
-        store_result(1)
+        low, high = (0, PACK // 2), (PACK // 2, PACK)
+        empty(0, 0, nc.scalar.copy)
+        store(*low, places(0))
+        empty(1, 0, nc.scalar.copy)
+        store(*low, places(1))
+        empty(0, 1, nc.scalar.copy)
+        empty(1, 1, nc.vector.tensor_copy)
+        store(*high, slice(0, HALF))
         round_result(0)
         round_result(1)
-        quantise_result(0)
-        store_result(2)
-        store_result(3)
-        quantise_result(1)
-        nc.sync.dma_start(out=words(out_1)[:, :HALF], in_=y_codes[:, :HALF].bitcast(I32))
+        empty(2, 0, nc.scalar.copy)
+        empty(3, 0, nc.scalar.copy)
+        store(*low, slice(HALF, S))
+        empty(3, 1, nc.scalar.copy)
+        store(*high, slice(HALF, S))
         round_result(2)
+        quantise_result(0, 2)
         round_result(3)
-        quantise_result(2)
-        quantise_result(3)
-        nc.sync.dma_start(out=words(out_1)[:, HALF:], in_=y_codes[:, HALF:].bitcast(I32))
+        quantise_result(2, 3)
+        quantise_result(3, 4)
+        nc.sync.dma_start(out=words(out_1), in_=y_codes[:].bitcast(I32))
         for g in range(P // QUADRANT):
             queue = nc.sync if g % 2 == 0 else nc.scalar
             queue.dma_start(

@@ -189,7 +189,7 @@ def tile_picked_phlora_none_po_kernel(
         h_acc = {}
         y_acc = {}
 
-        y_banks = (("y_acc0", "y_other0"), ("y_acc1", "y_other1"), ("h_acc2",), ("h_acc3", "h_acc1"))
+        y_banks = (("y_acc0", "y_other0"), ("y_acc1", "y_other1"), ("h_acc2", "h_acc1"), ("h_acc3", "h_acc0"))
 
         def product(bank, t, w, w_plane, moving, moving_plane, start, stop):
             nc.tensor.matmul_mx(
@@ -216,21 +216,14 @@ def tile_picked_phlora_none_po_kernel(
         def quantise_hidden(c):
             nc.vector.quantize_mx(out=h_codes[c][:].bitcast(FP8X4), scales=h_plane[c][:], in_=h_bf[c][:])
 
-        def direct(c):
-            y_acc[c] = [
-                psum.tile([P, PACK * CHUNK], F32, name="y_acc%d_%d" % (c, u), tag=tag)
-                for u, tag in enumerate(y_banks[c])
-            ]
-            per_bank = PACK // len(y_acc[c])
-            for t in range(PACK):
-                opens = t % per_bank == 0
-                product(y_acc[c][t // per_bank], t, w1_dealt, w1_plane, picked(c), x_plane[:, places(c)], opens, False)
+        def direct(c, u):
+            y_acc[c, u] = psum.tile([P, PACK * CHUNK], F32, name="y_acc%d_%d" % (c, u), tag=y_banks[c][u])
+            for t in (2 * u, 2 * u + 1):
+                product(y_acc[c, u], t, w1_dealt, w1_plane, picked(c), x_plane[:, places(c)], t == 2 * u, False)
 
-        def adapter(c):
-            per_bank = PACK // len(y_acc[c])
-            for t in range(PACK):
-                closes = t % per_bank == per_bank - 1
-                product(y_acc[c][t // per_bank], t, w3_dealt, w3_plane, h_codes[c][:], h_plane[c][:], False, closes)
+        def adapter(c, u):
+            for t in (2 * u, 2 * u + 1):
+                product(y_acc[c, u], t, w3_dealt, w3_plane, h_codes[c][:], h_plane[c][:], False, t == 2 * u + 1)
 
         def store(first, last, cols):
             g = cols.start // HALF
@@ -240,9 +233,8 @@ def tile_picked_phlora_none_po_kernel(
             )
 
         def empty(c, u, copy):
-            per_bank = PACK // len(y_acc[c])
-            rows = slice(u * per_bank, (u + 1) * per_bank)
-            copy(out=y[c][:, rows], in_=y_acc[c][u][:].rearrange("p (t n) -> p t n", t=PACK)[:, rows])
+            rows = slice(2 * u, 2 * u + 2)
+            copy(out=y[c][:, rows], in_=y_acc[c, u][:].rearrange("p (t n) -> p t n", t=PACK)[:, rows])
 
         def round_result(c):
             dst = y_bf[c].rearrange("p (n i t) -> p n t i", i=4, t=PACK)
@@ -261,43 +253,53 @@ def tile_picked_phlora_none_po_kernel(
         deal(w3_dealt, w3_raw)
         for c in chunks:
             hidden(c)
-        direct(0)
-        direct(1)
+        direct(0, 0)
+        direct(1, 0)
+        direct(0, 1)
         round_hidden(0, nc.scalar.copy)
         round_hidden(1, nc.vector.tensor_copy)
         quantise_hidden(0)
-        adapter(0)
+        adapter(0, 0)
+        direct(1, 1)
         round_hidden(2, nc.scalar.copy)
         quantise_hidden(1)
-        adapter(1)
+        adapter(1, 0)
+        adapter(0, 1)
+        adapter(1, 1)
         round_hidden(3, nc.vector.tensor_copy)
         quantise_hidden(2)
         quantise_hidden(3)
-        direct(2)
-        adapter(2)
-        direct(3)
-        adapter(3)
+        direct(2, 0)
+        adapter(2, 0)
+        direct(2, 1)
+        adapter(2, 1)
+        direct(3, 0)
+        adapter(3, 0)
+        direct(3, 1)
+        adapter(3, 1)
         low, high = (0, PACK // 2), (PACK // 2, PACK)
         empty(0, 0, nc.scalar.copy)
         store(*low, places(0))
         empty(1, 0, nc.scalar.copy)
         store(*low, places(1))
         empty(0, 1, nc.scalar.copy)
-        empty(1, 1, nc.vector.tensor_copy)
+        empty(1, 1, nc.scalar.copy)
         store(*high, slice(0, HALF))
         round_result(0)
-        round_result(1)
         empty(2, 0, nc.scalar.copy)
+        empty(2, 1, nc.vector.tensor_copy)
+        round_result(1)
         empty(3, 0, nc.scalar.copy)
         store(*low, slice(HALF, S))
         empty(3, 1, nc.scalar.copy)
         store(*high, slice(HALF, S))
         round_result(2)
         quantise_result(0, 2)
+        nc.sync.dma_start(out=words(out_1)[:, :HALF], in_=y_codes[:, :HALF].bitcast(I32))
         round_result(3)
         quantise_result(2, 3)
         quantise_result(3, 4)
-        nc.sync.dma_start(out=words(out_1), in_=y_codes[:].bitcast(I32))
+        nc.sync.dma_start(out=words(out_1)[:, HALF:], in_=y_codes[:, HALF:].bitcast(I32))
         for g in range(P // QUADRANT):
             queue = nc.sync if g % 2 == 0 else nc.scalar
             queue.dma_start(

@@ -24,7 +24,7 @@ QUADRANT = 32
 BLOCK_ROWS = 8
 
 W2_LEAD = 3
-W2_ON_SCALAR = 24
+W2_ON_SCALAR = (52, 40)
 Y_ON_SCALAR = (0, 0, 0, 32)
 WARM_WIDTHS = (256, 256, 512, 512)
 
@@ -50,8 +50,7 @@ def tile_picked_phlora_none_po_kernel(
         offsets = keep.tile([P, S // LIST_ROWS], U16, name="offsets")
         xs_win = tile("xs_win", T, U8)
         ws_raw = tile("ws_raw", 2 * H, U8)
-        x_plane = tile("x_plane", S, U8)
-        w_planes = shared.tile([P, 2 * H], U8, name="w_planes", align_bytes=64, offset=0)
+        w_planes = shared.tile([P, 2 * H], U8, name="w_planes", align_bytes=64, offset=2 * PACK * HALF)
         x_win = tile("x_win", T, U32, tag="x_then_w")
 
         nc.vector.memset(xs_win[:].bitcast(I32), 0)
@@ -93,11 +92,6 @@ def tile_picked_phlora_none_po_kernel(
                 )
 
         nc.vector.tensor_copy(xs_got[:], xs_win[:].indirect(offsets[:]))
-        nc.vector.tensor_copy(out=x_plane[:].bitcast(I32), in_=xs_got[:].bitcast(I32))
-        place_rows(x_plane)
-        w3_words_raw = tile("w3_raw", H, I32, tag="xs_then_w")
-        w3_raw = w3_words_raw[:]
-        nc.sync.dma_start(out=w3_raw, in_=words(w3_words))
 
         m_half = HALF // PACK
         w2_codes = tile("w2_codes", H, U32)
@@ -109,9 +103,20 @@ def tile_picked_phlora_none_po_kernel(
         ]
         w2_src = [raw[:].rearrange("p (j m t) -> p m j t", j=PACK, t=PACK) for raw in w2_raw]
         w2_dst = [bf[:].rearrange("p (t m j) -> p m j t", j=PACK, t=PACK) for bf in w2_bf]
-        nc.scalar.copy(out=w2_dst[0][:, :m_half], in_=w2_src[0][:, :m_half])
-        nc.scalar.copy(out=w2_dst[1][:, :W2_ON_SCALAR], in_=w2_src[1][:, :W2_ON_SCALAR])
-        nc.vector.tensor_copy(out=w2_dst[1][:, W2_ON_SCALAR:], in_=w2_src[1][:, W2_ON_SCALAR:])
+
+        def round_w2(a):
+            share = W2_ON_SCALAR[a]
+            nc.scalar.copy(out=w2_dst[a][:, :share], in_=w2_src[a][:, :share])
+            nc.vector.tensor_copy(out=w2_dst[a][:, share:], in_=w2_src[a][:, share:])
+
+        round_w2(0)
+        x_plane = tile("x_plane", S, U8, tag="w2_raw0")
+        nc.vector.tensor_copy(out=x_plane[:].bitcast(I32), in_=xs_got[:].bitcast(I32))
+        place_rows(x_plane)
+        w3_words_raw = tile("w3_raw", H, I32, tag="xs_then_w")
+        w3_raw = w3_words_raw[:]
+        nc.sync.dma_start(out=w3_raw, in_=words(w3_words))
+        round_w2(1)
         for pair in range(2):
             for a in range(2):
                 for t in (2 * pair, 2 * pair + 1):
@@ -143,7 +148,7 @@ def tile_picked_phlora_none_po_kernel(
             )
 
         x_got = [
-            shared.tile([P, HALF], U32, name="x_got%d" % a, align_bytes=64, offset=w2_bf_bytes + 4 * HALF * a)
+            shared.tile([P, HALF], U32, name="x_got%d" % a, align_bytes=64, offset=(w2_bf_bytes + 4 * HALF) * (1 - a))
             for a in range(2)
         ]
         list_cols = HALF // LIST_ROWS

@@ -23,10 +23,10 @@ LIST_ROWS = 16
 QUADRANT = 32
 BLOCK_ROWS = 8
 
-W2_LEAD = 3
-W2_ON_SCALAR = (52, 40)
+W2_ON_SCALAR = 60
 Y_ON_SCALAR = (0, 0, 0, 32)
-WARM_WIDTHS = (256, 256, 512, 512)
+WARM_ROWS = 32
+WARM_WIDTHS = (128, 128, 128, 512, 512)
 
 FLOPS = 3 * 2 * 512 * 512 * 512
 
@@ -49,8 +49,7 @@ def tile_picked_phlora_none_po_kernel(
 
         offsets = keep.tile([P, S // LIST_ROWS], U16, name="offsets")
         xs_win = tile("xs_win", T, U8)
-        ws_raw = tile("ws_raw", 2 * H, U8)
-        w_planes = shared.tile([P, 2 * H], U8, name="w_planes", align_bytes=64, offset=2 * PACK * HALF)
+        ws_raw = tile("ws_raw", H, U8, tag="ws_then_w3")
         x_win = tile("x_win", T, U32, tag="x_then_w")
 
         nc.vector.memset(xs_win[:].bitcast(I32), 0)
@@ -61,100 +60,77 @@ def tile_picked_phlora_none_po_kernel(
         nc.gpsimd.memset(seed[:], 0.0)
         nc.scalar.copy(out=seed_bf[:], in_=seed[:])
 
-        w2_rows = w2.rearrange("(p j) c -> p j c", j=PACK)
-        w2_raw = [tile("w2_raw%d" % a, PACK * HALF, F32) for a in range(2)]
-
-        def load_w2(a, first, last):
-            nc.sync.dma_start(
-                out=w2_raw[a][:, first * HALF : last * HALF].rearrange("p (j c) -> p j c", c=HALF),
-                in_=w2_rows[:, first:last, a * HALF : (a + 1) * HALF],
-            )
-
-        load_w2(0, 0, W2_LEAD)
+        w2_rows = w2.rearrange("(p j) c -> p (j c)", j=PACK)
+        w2_raw = tile("w2_raw", PACK * H, F32)
+        nc.sync.dma_start(out=w2_raw[:, :H], in_=w2_rows[:, :H])
         nc.sync.dma_start(offsets[:], offs)
         nc.sync.dma_start(out=xs_win[0:P:BLOCK_ROWS, :].bitcast(I32), in_=x_scales[0].bitcast(I32))
+        nc.sync.dma_start(out=w2_raw[:, H : 2 * H], in_=w2_rows[:, H : 2 * H])
         for w, rows in enumerate((w1_scales, w3_scales)):
-            nc.sync.dma_start(out=ws_raw[0:P:BLOCK_ROWS, w * H : (w + 1) * H].bitcast(I32), in_=rows[0].bitcast(I32))
-        load_w2(0, W2_LEAD, PACK)
-        load_w2(1, 0, PACK)
+            nc.sync.dma_start(out=ws_raw[PACK * w : P : BLOCK_ROWS, :].bitcast(I32), in_=rows[0].bitcast(I32))
+        nc.sync.dma_start(out=w2_raw[:, 2 * H :], in_=w2_rows[:, 2 * H :])
         nc.sync.dma_start(out=x_win[:].bitcast(I32), in_=words(x_words))
-        w1_words_raw = tile("w1_raw", H, U32)
-        w1_raw = w1_words_raw[:]
-        nc.sync.dma_start(out=w1_raw.bitcast(I32), in_=words(w1_words))
+        w1_raw = tile("w1_raw", H, U32)
+        nc.sync.dma_start(out=w1_raw[:].bitcast(I32), in_=words(w1_words))
 
-        xs_got = tile("xs_got", S, U8, tag="xs_then_w")
-
-        def place_rows(plane):
-            for j in range(1, PACK):
-                nc.sync.dma_start(
-                    out=plane[j:P:QUADRANT, :].bitcast(I32),
-                    in_=plane[BLOCK_ROWS * j : P : QUADRANT, :].bitcast(I32),
-                )
-
+        xs_got = tile("xs_got", S, U8)
         nc.vector.tensor_copy(xs_got[:], xs_win[:].indirect(offsets[:]))
 
-        m_half = HALF // PACK
         w2_codes = tile("w2_codes", H, U32)
         w2_plane = tile("w2_plane", H, U8)
-        w2_bf_bytes = 2 * PACK * HALF
-        w2_bf = [
-            shared.tile([P, PACK * HALF], BF16, name="w2_bf%d" % a, align_bytes=64, offset=w2_bf_bytes * a)
-            for a in range(2)
-        ]
-        w2_src = [raw[:].rearrange("p (j m t) -> p m j t", j=PACK, t=PACK) for raw in w2_raw]
-        w2_dst = [bf[:].rearrange("p (t m j) -> p m j t", j=PACK, t=PACK) for bf in w2_bf]
+        w2_bf = shared.tile([P, PACK * H], BF16, name="w2_bf", align_bytes=64, offset=0)
+        w2_dst = w2_bf[:].rearrange("p (t m j) -> p m j t", j=PACK, t=PACK)
 
-        def round_w2(a):
-            share = W2_ON_SCALAR[a]
-            nc.scalar.copy(out=w2_dst[a][:, :share], in_=w2_src[a][:, :share])
-            nc.vector.tensor_copy(out=w2_dst[a][:, share:], in_=w2_src[a][:, share:])
+        w2_src = w2_raw[:].rearrange("p (j m t) -> p m j t", j=PACK, t=PACK)
+        for a in range(2):
+            rows = slice(2 * a, 2 * a + 2)
+            nc.scalar.copy(out=w2_dst[:, :W2_ON_SCALAR, rows], in_=w2_src[:, :W2_ON_SCALAR, rows])
 
-        round_w2(0)
-        x_plane = tile("x_plane", S, U8, tag="w2_raw0")
-        nc.vector.tensor_copy(out=x_plane[:].bitcast(I32), in_=xs_got[:].bitcast(I32))
-        place_rows(x_plane)
-        w3_words_raw = tile("w3_raw", H, I32, tag="xs_then_w")
-        w3_raw = w3_words_raw[:]
-        nc.sync.dma_start(out=w3_raw, in_=words(w3_words))
-        round_w2(1)
-        for pair in range(2):
-            for a in range(2):
-                for t in (2 * pair, 2 * pair + 1):
-                    cols = slice(t * P + a * m_half, t * P + (a + 1) * m_half)
-                    nc.vector.quantize_mx(
-                        out=w2_codes[:, cols].bitcast(FP8X4),
-                        scales=w2_plane[:, cols],
-                        in_=w2_bf[a][:, t * HALF : (t + 1) * HALF],
-                    )
+        planes = tile("planes", S + H, U8)
+        dealt_bytes = planes[:, S:].rearrange("p (t m) -> p t m", t=PACK)
+        raw_bytes = ws_raw[:].rearrange("p (m t) -> p t m", t=PACK)
+        nc.vector.tensor_copy(out=dealt_bytes[:, :2], in_=raw_bytes[:, :2])
+        nc.vector.tensor_copy(out=planes[:, :S].bitcast(I32), in_=xs_got[:].bitcast(I32))
+        nc.vector.tensor_copy(out=dealt_bytes[:, 2:], in_=raw_bytes[:, 2:])
 
-        nc.vector.tensor_copy(
-            out=w_planes[:].rearrange("p (w t m) -> p w t m", w=2, t=PACK),
-            in_=ws_raw[:].rearrange("p (w m t) -> p w t m", w=2, t=PACK),
-        )
-        place_rows(w_planes)
-        w1_plane = w_planes[:, 0:H]
-        w3_plane = w_planes[:, H:]
+        def place_rows(first, cols):
+            for j in range(1, PACK):
+                nc.sync.dma_start(
+                    out=planes[first + j : P : QUADRANT, cols].bitcast(I32),
+                    in_=planes[first + BLOCK_ROWS * j : P : QUADRANT, cols].bitcast(I32),
+                )
+
+        place_rows(0, slice(0, S + H))
+        x_plane = planes[:, :S]
+        w1_plane = planes[:, S:]
+        w3_plane = planes[PACK:, S:]
+        w3_raw = tile("w3_raw", H, I32, tag="ws_then_w3")
+        nc.sync.dma_start(out=w3_raw[:], in_=words(w3_words))
+        place_rows(PACK, slice(S, S + H))
+        nc.vector.tensor_copy(out=w2_dst[:, W2_ON_SCALAR:], in_=w2_src[:, W2_ON_SCALAR:])
+        for cols in (slice(0, P), slice(P, H)):
+            nc.vector.quantize_mx(
+                out=w2_codes[:, cols].bitcast(FP8X4),
+                scales=w2_plane[:, cols],
+                in_=w2_bf[:, PACK * cols.start : PACK * cols.stop],
+            )
 
         warm = psum.tile([P, H], F32, name="warm", tag="y_acc0")
         for width in WARM_WIDTHS:
             nc.tensor.matmul_mx(
-                out=warm[:, :width],
-                lhsT=w2_codes[:, 0:P].bitcast(FP8X4),
-                lhsT_scale=w2_plane[:, 0:P],
+                out=warm[:WARM_ROWS, :width],
+                lhsT=w2_codes[:, :WARM_ROWS].bitcast(FP8X4),
+                lhsT_scale=w2_plane[:, :WARM_ROWS],
                 rhs=w2_codes[:, :width].bitcast(FP8X4),
                 rhs_scale=w2_plane[:, :width],
                 start=True,
                 stop=True,
             )
 
-        x_got = [
-            shared.tile([P, HALF], U32, name="x_got%d" % a, align_bytes=64, offset=(w2_bf_bytes + 4 * HALF) * (1 - a))
-            for a in range(2)
-        ]
+        x_got = [shared.tile([P, HALF], U32, name="x_got%d" % a, align_bytes=64, offset=4 * HALF * a) for a in range(2)]
         list_cols = HALF // LIST_ROWS
         for a in range(2):
             nc.vector.tensor_copy(x_got[a][:], x_win[:].indirect(offsets[:, list_cols * a : list_cols * (a + 1)]))
-
 
         def places(c):
             return slice(c * CHUNK, (c + 1) * CHUNK)
@@ -162,22 +138,17 @@ def tile_picked_phlora_none_po_kernel(
         def picked(c):
             return x_got[c // 2][:, places(c % 2)]
 
-        w_dealt = tile("w_dealt", 2 * H, I32, tag="x_then_w")
-        w1_dealt = w_dealt[:, 0:H]
-        w3_dealt = w_dealt[:, H:]
-
-        def deal(dealt, source):
-            nc.vector.tensor_copy(
+        def deal(copy, dealt, source):
+            copy(
                 out=dealt.rearrange("p (t m) -> p m t", t=PACK),
                 in_=source.rearrange("p (m t) -> p m t", t=PACK),
             )
 
         w1_tile = tile("w1_dealt", H, U32)
         w1_dealt = w1_tile[:]
-        nc.scalar.copy(
-            out=w1_dealt.rearrange("p (t m) -> p m t", t=PACK),
-            in_=w1_raw.rearrange("p (m t) -> p m t", t=PACK),
-        )
+        w3_tile = tile("w3_dealt", H, I32, tag="x_then_w")
+        w3_dealt = w3_tile[:]
+        deal(nc.scalar.copy, w1_dealt, w1_raw[:])
 
         chunks = range(CHUNKS)
         h_bf = [tile("h_bf%d" % c, PACK * CHUNK, BF16, tag="h_bf1" if c == LAST else None) for c in chunks]
@@ -255,7 +226,7 @@ def tile_picked_phlora_none_po_kernel(
             rounded = y_bf_half[first // 2][:, (first % 2) * H : ((last - 1) % 2 + 1) * H]
             nc.vector.quantize_mx(out=y_codes[:, cols].bitcast(FP8X4), scales=y_plane[:, cols], in_=rounded)
 
-        deal(w3_dealt, w3_raw)
+        deal(nc.vector.tensor_copy, w3_dealt, w3_raw[:])
         for c in chunks:
             hidden(c)
         direct(0, 0)

@@ -24,7 +24,7 @@ QUADRANT = 32
 BLOCK_ROWS = 8
 
 W2_ON_SCALAR = 60
-Y_ON_SCALAR = (0, 0, 0, 32)
+Y_ON_SCALAR = (0, 0, 0, 12)
 WARM_ROWS = 32
 WARM_WIDTHS = (128, 128, 128, 512, 512)
 
@@ -151,7 +151,7 @@ def tile_picked_phlora_none_po_kernel(
         deal(nc.scalar.copy, w1_dealt, w1_raw[:])
 
         chunks = range(CHUNKS)
-        h_bf = [tile("h_bf%d" % c, PACK * CHUNK, BF16, tag="h_bf1" if c == LAST else None) for c in chunks]
+        h_bf = [tile("h_bf%d" % c, PACK * CHUNK, BF16) for c in chunks]
         h_codes = [tile("h_codes%d" % c, CHUNK, U32) for c in chunks]
         h_plane = [tile("h_plane%d" % c, CHUNK, U8) for c in chunks]
         y_tiles = [tile("y%d" % g, PACK * HALF, F32) for g in range(2)]
@@ -232,38 +232,32 @@ def tile_picked_phlora_none_po_kernel(
         direct(0, 0)
         direct(1, 0)
         direct(0, 1)
+        direct(1, 1)
         round_hidden(0, nc.scalar.copy)
         round_hidden(1, nc.vector.tensor_copy)
-        quantise_hidden(0)
-        adapter(0, 0)
-        direct(1, 1)
         round_hidden(2, nc.scalar.copy)
-        quantise_hidden(1)
+        round_hidden(3, nc.scalar.copy)
+        for c in chunks:
+            quantise_hidden(c)
+        adapter(0, 0)
         adapter(1, 0)
         adapter(0, 1)
         adapter(1, 1)
-        round_hidden(3, nc.vector.tensor_copy)
-        quantise_hidden(2)
-        quantise_hidden(3)
-        direct(2, 0)
-        adapter(2, 0)
-        direct(2, 1)
-        adapter(2, 1)
-        direct(3, 0)
-        adapter(3, 0)
-        direct(3, 1)
-        adapter(3, 1)
+        for c in (2, 3):
+            for u in range(2):
+                direct(c, u)
+                adapter(c, u)
         low, high = (0, PACK // 2), (PACK // 2, PACK)
         empty(0, 0, nc.scalar.copy)
         store(*low, places(0))
         empty(1, 0, nc.scalar.copy)
         store(*low, places(1))
-        empty(0, 1, nc.scalar.copy)
+        empty(0, 1, nc.vector.tensor_copy)
         empty(1, 1, nc.scalar.copy)
         store(*high, slice(0, HALF))
         round_result(0)
         empty(2, 0, nc.scalar.copy)
-        empty(2, 1, nc.vector.tensor_copy)
+        empty(2, 1, nc.scalar.copy)
         round_result(1)
         empty(3, 0, nc.scalar.copy)
         store(*low, slice(HALF, S))

@@ -23,10 +23,10 @@ LIST_ROWS = 16
 QUADRANT = 32
 BLOCK_ROWS = 8
 
-W2_ON_SCALAR = 60
+W2_ON_SCALAR = 42
 Y_ON_SCALAR = (0, 0, 0, 12)
 WARM_ROWS = 32
-WARM_WIDTHS = (128, 128, 128, 512, 512)
+WARM_WIDTHS = (128, 128, 128, 128, 512, 512)
 
 FLOPS = 3 * 2 * 512 * 512 * 512
 
@@ -49,11 +49,16 @@ def tile_picked_phlora_none_po_kernel(
 
         offsets = keep.tile([P, S // LIST_ROWS], U16, name="offsets")
         xs_win = tile("xs_win", T, U8)
-        ws_raw = tile("ws_raw", H, U8, tag="ws_then_w3")
+        ws_raw = tile("ws_raw", 2 * H, U8)
         x_win = tile("x_win", T, U32, tag="x_then_w")
 
         nc.vector.memset(xs_win[:].bitcast(I32), 0)
         nc.gpsimd.memset(ws_raw[:].bitcast(I32), 0)
+
+        for w, rows in enumerate((w1_scales, w3_scales)):
+            nc.scalar.dma_start(
+                out=ws_raw[0:P:BLOCK_ROWS, w * H : (w + 1) * H].bitcast(I32), in_=rows[0].bitcast(I32)
+            )
 
         seed = tile("seed", 16, F32)
         seed_bf = tile("seed_bf", 16, BF16)
@@ -66,14 +71,17 @@ def tile_picked_phlora_none_po_kernel(
         nc.sync.dma_start(offsets[:], offs)
         nc.sync.dma_start(out=xs_win[0:P:BLOCK_ROWS, :].bitcast(I32), in_=x_scales[0].bitcast(I32))
         nc.sync.dma_start(out=w2_raw[:, H : 2 * H], in_=w2_rows[:, H : 2 * H])
-        for w, rows in enumerate((w1_scales, w3_scales)):
-            nc.sync.dma_start(out=ws_raw[PACK * w : P : BLOCK_ROWS, :].bitcast(I32), in_=rows[0].bitcast(I32))
         nc.sync.dma_start(out=w2_raw[:, 2 * H :], in_=w2_rows[:, 2 * H :])
         nc.sync.dma_start(out=x_win[:].bitcast(I32), in_=words(x_words))
         w1_raw = tile("w1_raw", H, U32)
         nc.sync.dma_start(out=w1_raw[:].bitcast(I32), in_=words(w1_words))
 
-        xs_got = tile("xs_got", S, U8)
+        planes = tile("planes", S + 2 * H, U8)
+        nc.vector.tensor_copy(
+            out=planes[:, S:].rearrange("p (w t m) -> p w t m", w=2, t=PACK),
+            in_=ws_raw[:].rearrange("p (w m t) -> p w t m", w=2, t=PACK),
+        )
+        xs_got = tile("xs_got", S, U8, tag="xs_then_w3")
         nc.vector.tensor_copy(xs_got[:], xs_win[:].indirect(offsets[:]))
 
         w2_codes = tile("w2_codes", H, U32)
@@ -84,14 +92,10 @@ def tile_picked_phlora_none_po_kernel(
         w2_src = w2_raw[:].rearrange("p (j m t) -> p m j t", j=PACK, t=PACK)
         for a in range(2):
             rows = slice(2 * a, 2 * a + 2)
-            nc.scalar.copy(out=w2_dst[:, :W2_ON_SCALAR, rows], in_=w2_src[:, :W2_ON_SCALAR, rows])
+            nc.scalar.copy(out=w2_dst[:, :, rows, 0], in_=w2_src[:, :, rows, 0])
+            nc.scalar.copy(out=w2_dst[:, :W2_ON_SCALAR, rows, 1:], in_=w2_src[:, :W2_ON_SCALAR, rows, 1:])
 
-        planes = tile("planes", S + H, U8)
-        dealt_bytes = planes[:, S:].rearrange("p (t m) -> p t m", t=PACK)
-        raw_bytes = ws_raw[:].rearrange("p (m t) -> p t m", t=PACK)
-        nc.vector.tensor_copy(out=dealt_bytes[:, :2], in_=raw_bytes[:, :2])
         nc.vector.tensor_copy(out=planes[:, :S].bitcast(I32), in_=xs_got[:].bitcast(I32))
-        nc.vector.tensor_copy(out=dealt_bytes[:, 2:], in_=raw_bytes[:, 2:])
 
         def place_rows(first, cols):
             for j in range(1, PACK):
@@ -100,14 +104,13 @@ def tile_picked_phlora_none_po_kernel(
                     in_=planes[first + BLOCK_ROWS * j : P : QUADRANT, cols].bitcast(I32),
                 )
 
-        place_rows(0, slice(0, S + H))
+        place_rows(0, slice(0, S + 2 * H))
         x_plane = planes[:, :S]
-        w1_plane = planes[:, S:]
-        w3_plane = planes[PACK:, S:]
-        w3_raw = tile("w3_raw", H, I32, tag="ws_then_w3")
+        w1_plane = planes[:, S : S + H]
+        w3_plane = planes[:, S + H :]
+        w3_raw = tile("w3_raw", H, I32, tag="xs_then_w3")
         nc.sync.dma_start(out=w3_raw[:], in_=words(w3_words))
-        place_rows(PACK, slice(S, S + H))
-        nc.vector.tensor_copy(out=w2_dst[:, W2_ON_SCALAR:], in_=w2_src[:, W2_ON_SCALAR:])
+        nc.vector.tensor_copy(out=w2_dst[:, W2_ON_SCALAR:, :, 1:], in_=w2_src[:, W2_ON_SCALAR:, :, 1:])
         for cols in (slice(0, P), slice(P, H)):
             nc.vector.quantize_mx(
                 out=w2_codes[:, cols].bitcast(FP8X4),

@@ -45,7 +45,7 @@ def tile_picked_phlora_none_po_kernel(
         psum = ctx.enter_context(tc.psum_pool(name="psum", bufs=1))
 
         def tile(name, cols, dtype, tag=None):
-            return keep.tile([P, cols], dtype, name=name, tag=tag or name, align_bytes=64)
+            return keep.tile([P, cols], dtype, name=name, tag=tag or name, align_bytes=256)
 
         offsets = keep.tile([P, S // LIST_ROWS], U16, name="offsets")
         xs_win = tile("xs_win", T, U8)
@@ -86,7 +86,7 @@ def tile_picked_phlora_none_po_kernel(
 
         w2_codes = tile("w2_codes", H, U32)
         w2_plane = tile("w2_plane", H, U8)
-        w2_bf = shared.tile([P, PACK * H], BF16, name="w2_bf", align_bytes=64, offset=0)
+        w2_bf = shared.tile([P, PACK * H], BF16, name="w2_bf", align_bytes=256, offset=0)
         w2_dst = w2_bf[:].rearrange("p (t m j) -> p m j t", j=PACK, t=PACK)
 
         w2_src = w2_raw[:].rearrange("p (j m t) -> p m j t", j=PACK, t=PACK)
@@ -130,7 +130,7 @@ def tile_picked_phlora_none_po_kernel(
                 stop=True,
             )
 
-        x_got = [shared.tile([P, HALF], U32, name="x_got%d" % a, align_bytes=64, offset=4 * HALF * a) for a in range(2)]
+        x_got = [shared.tile([P, HALF], U32, name="x_got%d" % a, align_bytes=256, offset=4 * HALF * a) for a in range(2)]
         list_cols = HALF // LIST_ROWS
         for a in range(2):
             nc.vector.tensor_copy(x_got[a][:], x_win[:].indirect(offsets[:, list_cols * a : list_cols * (a + 1)]))
@@ -195,10 +195,12 @@ def tile_picked_phlora_none_po_kernel(
         def quantise_hidden(c):
             nc.vector.quantize_mx(out=h_codes[c][:].bitcast(FP8X4), scales=h_plane[c][:], in_=h_bf[c][:])
 
-        def direct(c, u):
-            y_acc[c, u] = psum.tile([P, PACK * CHUNK], F32, name="y_acc%d_%d" % (c, u), tag=y_banks[c][u])
+        def direct(cs, u):
+            for c in cs:
+                y_acc[c, u] = psum.tile([P, PACK * CHUNK], F32, name="y_acc%d_%d" % (c, u), tag=y_banks[c][u])
             for t in (2 * u, 2 * u + 1):
-                product(y_acc[c, u], t, w1_dealt, w1_plane, picked(c), x_plane[:, places(c)], t == 2 * u, False)
+                for c in cs:
+                    product(y_acc[c, u], t, w1_dealt, w1_plane, picked(c), x_plane[:, places(c)], t == 2 * u, False)
 
         def adapter(c, u):
             for t in (2 * u, 2 * u + 1):
@@ -232,10 +234,8 @@ def tile_picked_phlora_none_po_kernel(
         deal(nc.vector.tensor_copy, w3_dealt, w3_raw[:])
         for c in chunks:
             hidden(c)
-        direct(0, 0)
-        direct(1, 0)
-        direct(0, 1)
-        direct(1, 1)
+        direct((0, 1), 0)
+        direct((0, 1), 1)
         round_hidden(0, nc.scalar.copy)
         round_hidden(1, nc.vector.tensor_copy)
         round_hidden(2, nc.scalar.copy)
@@ -248,7 +248,7 @@ def tile_picked_phlora_none_po_kernel(
         adapter(1, 1)
         for c in (2, 3):
             for u in range(2):
-                direct(c, u)
+                direct((c,), u)
                 adapter(c, u)
         low, high = (0, PACK // 2), (PACK // 2, PACK)
         empty(0, 0, nc.scalar.copy)

@@ -202,9 +202,10 @@ def tile_picked_phlora_none_po_kernel(
                 for c in cs:
                     product(y_acc[c, u], t, w1_dealt, w1_plane, picked(c), x_plane[:, places(c)], t == 2 * u, False)
 
-        def adapter(c, u):
+        def adapter(cs, u):
             for t in (2 * u, 2 * u + 1):
-                product(y_acc[c, u], t, w3_dealt, w3_plane, h_codes[c][:], h_plane[c][:], False, t == 2 * u + 1)
+                for c in cs:
+                    product(y_acc[c, u], t, w3_dealt, w3_plane, h_codes[c][:], h_plane[c][:], False, t == 2 * u + 1)
 
         def store(first, last, cols):
             g = cols.start // HALF
@@ -242,14 +243,13 @@ def tile_picked_phlora_none_po_kernel(
         round_hidden(3, nc.scalar.copy)
         for c in chunks:
             quantise_hidden(c)
-        adapter(0, 0)
-        adapter(1, 0)
-        adapter(0, 1)
-        adapter(1, 1)
+        adapter((0,), 0)
+        adapter((1,), 0)
+        adapter((0, 1), 1)
         for c in (2, 3):
             for u in range(2):
                 direct((c,), u)
-                adapter(c, u)
+                adapter((c,), u)
         low, high = (0, PACK // 2), (PACK // 2, PACK)
         empty(0, 0, nc.scalar.copy)
         store(*low, places(0))

@@ -23,7 +23,7 @@ LIST_ROWS = 16
 QUADRANT = 32
 BLOCK_ROWS = 8
 
-W2_ON_SCALAR = 42
+W2_ON_SCALAR = 34
 Y_ON_SCALAR = (0, 0, 0, 12)
 WARM_ROWS = 32
 WARM_WIDTHS = (128, 128, 128, 128, 512, 512)
@@ -77,10 +77,11 @@ def tile_picked_phlora_none_po_kernel(
         nc.sync.dma_start(out=w1_raw[:].bitcast(I32), in_=words(w1_words))
 
         planes = tile("planes", S + 2 * H, U8)
-        nc.vector.tensor_copy(
-            out=planes[:, S:].rearrange("p (w t m) -> p w t m", w=2, t=PACK),
-            in_=ws_raw[:].rearrange("p (w m t) -> p w t m", w=2, t=PACK),
-        )
+        for w, copy in enumerate((nc.vector.tensor_copy, nc.gpsimd.tensor_copy)):
+            copy(
+                out=planes[:, S + w * H : S + (w + 1) * H].rearrange("p (t m) -> p t m", t=PACK),
+                in_=ws_raw[:, w * H : (w + 1) * H].rearrange("p (m t) -> p t m", t=PACK),
+            )
         xs_got = tile("xs_got", S, U8, tag="xs_then_w3")
         nc.vector.tensor_copy(xs_got[:], xs_win[:].indirect(offsets[:]))
 

from contextlib import ExitStack

import concourse.mybir as mybir

F32 = mybir.dt.float32
BF16 = mybir.dt.bfloat16
I32 = mybir.dt.int32
U32 = mybir.dt.uint32
U16 = mybir.dt.uint16
U8 = mybir.dt.uint8
FP8X4 = mybir.dt.float8_e4m3fn_x4

P = 128
PACK = 4
T = 2048
S = 512
H = 512
HALF = 256
CHUNK = 128
CHUNKS = S // CHUNK
LAST = CHUNKS - 1
LIST_ROWS = 16
QUADRANT = 32
BLOCK_ROWS = 8

W2_ON_SCALAR = 34
Y_ON_SCALAR = (0, 0, 0, 12)
WARM_ROWS = 32
WARM_WIDTHS = (128, 128, 128, 128, 512, 512)

FLOPS = 3 * 2 * 512 * 512 * 512


def tile_picked_phlora_none_po_kernel(
    tc, x_words, x_scales, w1_words, w1_scales, w2, w3_words, w3_scales, offs, out_0, out_1, out_2
):
    nc = tc.nc

    def words(dram):
        return dram[0].rearrange("p c t -> p (c t)").bitcast(I32)

    with ExitStack() as ctx:
        keep = ctx.enter_context(tc.tile_pool(name="keep", bufs=1))
        shared = ctx.enter_context(tc.tile_pool(name="shared", bufs=1))
        psum = ctx.enter_context(tc.psum_pool(name="psum", bufs=1))

        def tile(name, cols, dtype, tag=None):
            return keep.tile([P, cols], dtype, name=name, tag=tag or name, align_bytes=256)

        offsets = keep.tile([P, S // LIST_ROWS], U16, name="offsets")
        xs_win = tile("xs_win", T, U8)
        ws_raw = tile("ws_raw", 2 * H, U8)
        x_win = tile("x_win", T, U32, tag="x_then_w")

        nc.vector.memset(xs_win[:].bitcast(I32), 0)
        nc.gpsimd.memset(ws_raw[:].bitcast(I32), 0)

        for w, rows in enumerate((w1_scales, w3_scales)):
            nc.scalar.dma_start(
                out=ws_raw[0:P:BLOCK_ROWS, w * H : (w + 1) * H].bitcast(I32), in_=rows[0].bitcast(I32)
            )

        seed = tile("seed", 16, F32)
        seed_bf = tile("seed_bf", 16, BF16)
        nc.gpsimd.memset(seed[:], 0.0)
        nc.scalar.copy(out=seed_bf[:], in_=seed[:])

        w2_rows = w2.rearrange("(p j) c -> p (j c)", j=PACK)
        w2_raw = tile("w2_raw", PACK * H, F32)
        nc.sync.dma_start(out=w2_raw[:, :H], in_=w2_rows[:, :H])
        nc.sync.dma_start(offsets[:], offs)
        nc.sync.dma_start(out=xs_win[0:P:BLOCK_ROWS, :].bitcast(I32), in_=x_scales[0].bitcast(I32))
        nc.sync.dma_start(out=w2_raw[:, H : 2 * H], in_=w2_rows[:, H : 2 * H])
        nc.sync.dma_start(out=w2_raw[:, 2 * H :], in_=w2_rows[:, 2 * H :])
        nc.sync.dma_start(out=x_win[:].bitcast(I32), in_=words(x_words))
        w1_raw = tile("w1_raw", H, U32)
        nc.sync.dma_start(out=w1_raw[:].bitcast(I32), in_=words(w1_words))

        planes = tile("planes", S + 2 * H, U8)
        for w, copy in enumerate((nc.vector.tensor_copy, nc.gpsimd.tensor_copy)):
            copy(
                out=planes[:, S + w * H : S + (w + 1) * H].rearrange("p (t m) -> p t m", t=PACK),
                in_=ws_raw[:, w * H : (w + 1) * H].rearrange("p (m t) -> p t m", t=PACK),
            )
        xs_got = tile("xs_got", S, U8, tag="xs_then_w3")
        nc.vector.tensor_copy(xs_got[:], xs_win[:].indirect(offsets[:]))

        w2_codes = tile("w2_codes", H, U32)
        w2_plane = tile("w2_plane", H, U8)
        w2_bf = shared.tile([P, PACK * H], BF16, name="w2_bf", align_bytes=256, offset=0)
        w2_dst = w2_bf[:].rearrange("p (t m j) -> p m j t", j=PACK, t=PACK)

        w2_src = w2_raw[:].rearrange("p (j m t) -> p m j t", j=PACK, t=PACK)
        for a in range(2):
            rows = slice(2 * a, 2 * a + 2)
            nc.scalar.copy(out=w2_dst[:, :, rows, 0], in_=w2_src[:, :, rows, 0])
            nc.scalar.copy(out=w2_dst[:, :W2_ON_SCALAR, rows, 1:], in_=w2_src[:, :W2_ON_SCALAR, rows, 1:])

        nc.vector.tensor_copy(out=planes[:, :S].bitcast(I32), in_=xs_got[:].bitcast(I32))

        def place_rows(first, cols):
            for j in range(1, PACK):
                nc.sync.dma_start(
                    out=planes[first + j : P : QUADRANT, cols].bitcast(I32),
                    in_=planes[first + BLOCK_ROWS * j : P : QUADRANT, cols].bitcast(I32),
                )

        place_rows(0, slice(0, S + 2 * H))
        x_plane = planes[:, :S]
        w1_plane = planes[:, S : S + H]
        w3_plane = planes[:, S + H :]
        w3_raw = tile("w3_raw", H, I32, tag="xs_then_w3")
        nc.sync.dma_start(out=w3_raw[:], in_=words(w3_words))
        nc.vector.tensor_copy(out=w2_dst[:, W2_ON_SCALAR:, :, 1:], in_=w2_src[:, W2_ON_SCALAR:, :, 1:])
        for cols in (slice(0, P), slice(P, H)):
            nc.vector.quantize_mx(
                out=w2_codes[:, cols].bitcast(FP8X4),
                scales=w2_plane[:, cols],
                in_=w2_bf[:, PACK * cols.start : PACK * cols.stop],
            )

        warm = psum.tile([P, H], F32, name="warm", tag="y_acc0")
        for width in WARM_WIDTHS:
            nc.tensor.matmul_mx(
                out=warm[:WARM_ROWS, :width],
                lhsT=w2_codes[:, :WARM_ROWS].bitcast(FP8X4),
                lhsT_scale=w2_plane[:, :WARM_ROWS],
                rhs=w2_codes[:, :width].bitcast(FP8X4),
                rhs_scale=w2_plane[:, :width],
                start=True,
                stop=True,
            )

        x_got = [shared.tile([P, HALF], U32, name="x_got%d" % a, align_bytes=256, offset=4 * HALF * a) for a in range(2)]
        list_cols = HALF // LIST_ROWS
        for a in range(2):
            nc.vector.tensor_copy(x_got[a][:], x_win[:].indirect(offsets[:, list_cols * a : list_cols * (a + 1)]))

        def places(c):
            return slice(c * CHUNK, (c + 1) * CHUNK)

        def picked(c):
            return x_got[c // 2][:, places(c % 2)]

        def deal(copy, dealt, source):
            copy(
                out=dealt.rearrange("p (t m) -> p m t", t=PACK),
                in_=source.rearrange("p (m t) -> p m t", t=PACK),
            )

        w1_tile = tile("w1_dealt", H, U32)
        w1_dealt = w1_tile[:]
        w3_tile = tile("w3_dealt", H, I32, tag="x_then_w")
        w3_dealt = w3_tile[:]
        deal(nc.scalar.copy, w1_dealt, w1_raw[:])

        chunks = range(CHUNKS)
        h_bf = [tile("h_bf%d" % c, PACK * CHUNK, BF16) for c in chunks]
        h_codes = [tile("h_codes%d" % c, CHUNK, U32) for c in chunks]
        h_plane = [tile("h_plane%d" % c, CHUNK, U8) for c in chunks]
        y_tiles = [tile("y%d" % g, PACK * HALF, F32) for g in range(2)]
        y_half = [y_tile[:].rearrange("p (t n) -> p t n", t=PACK) for y_tile in y_tiles]
        y = [y_half[c // 2][:, :, places(c % 2)] for c in chunks]
        y_bf_half = [tile("y_bf%d" % g, PACK * HALF, BF16) for g in range(2)]
        y_bf = [y_bf_half[c // 2][:, (c % 2) * H : (c % 2 + 1) * H] for c in chunks]
        y_codes = tile("y_codes", S, U32)
        y_plane = tile("y_plane", S, U8)
        y_rows = out_0.rearrange("(p t) c -> p t c", t=PACK)
        h_acc = {}
        y_acc = {}

        y_banks = (("y_acc0", "y_other0"), ("y_acc1", "y_other1"), ("h_acc2", "h_acc1"), ("h_acc3", "h_acc0"))

        def product(bank, t, w, w_plane, moving, moving_plane, start, stop):
            nc.tensor.matmul_mx(
                out=bank[:, t * CHUNK : (t + 1) * CHUNK],
                lhsT=w[:, t * P : (t + 1) * P].bitcast(FP8X4),
                lhsT_scale=w_plane[:, t * P : (t + 1) * P],
                rhs=moving.bitcast(FP8X4),
                rhs_scale=moving_plane,
                start=start,
                stop=stop,
            )

        def hidden(c):
            h_acc[c] = psum.tile([P, PACK * CHUNK], F32, name="h_acc%d" % c, tag="h_acc%d" % c)
            for t in range(PACK):
                product(h_acc[c], t, w2_codes, w2_plane, picked(c), x_plane[:, places(c)], True, True)

        def round_hidden(c, copy):
            copy(
                out=h_bf[c][:].rearrange("p (n t) -> p n t", t=PACK),
                in_=h_acc[c][:].rearrange("p (t n) -> p n t", t=PACK),
            )

        def quantise_hidden(c):
            nc.vector.quantize_mx(out=h_codes[c][:].bitcast(FP8X4), scales=h_plane[c][:], in_=h_bf[c][:])

        def direct(cs, u):
            for c in cs:
                y_acc[c, u] = psum.tile([P, PACK * CHUNK], F32, name="y_acc%d_%d" % (c, u), tag=y_banks[c][u])
            for t in (2 * u, 2 * u + 1):
                for c in cs:
                    product(y_acc[c, u], t, w1_dealt, w1_plane, picked(c), x_plane[:, places(c)], t == 2 * u, False)

        def adapter(cs, u):
            for t in (2 * u, 2 * u + 1):
                for c in cs:
                    product(y_acc[c, u], t, w3_dealt, w3_plane, h_codes[c][:], h_plane[c][:], False, t == 2 * u + 1)

        def store(first, last, cols):
            g = cols.start // HALF
            nc.sync.dma_start(
                out=y_rows[:, first:last, cols],
                in_=y_half[g][:, first:last, cols.start - g * HALF : cols.stop - g * HALF],
            )

        def empty(c, u, copy):
            rows = slice(2 * u, 2 * u + 2)
            copy(out=y[c][:, rows], in_=y_acc[c, u][:].rearrange("p (t n) -> p t n", t=PACK)[:, rows])

        def round_result(c):
            dst = y_bf[c].rearrange("p (n i t) -> p n t i", i=4, t=PACK)
            src = y[c].rearrange("p t (n i) -> p n t i", i=4)
            share = Y_ON_SCALAR[c]
            if share:
                nc.scalar.copy(out=dst[:, :share], in_=src[:, :share])
            if share < CHUNK // 4:
                nc.vector.tensor_copy(out=dst[:, share:], in_=src[:, share:])

        def quantise_result(first, last):
            cols = slice(first * CHUNK, last * CHUNK)
            rounded = y_bf_half[first // 2][:, (first % 2) * H : ((last - 1) % 2 + 1) * H]
            nc.vector.quantize_mx(out=y_codes[:, cols].bitcast(FP8X4), scales=y_plane[:, cols], in_=rounded)

        deal(nc.vector.tensor_copy, w3_dealt, w3_raw[:])
        for c in chunks:
            hidden(c)
        direct((0, 1), 0)
        direct((0, 1), 1)
        round_hidden(0, nc.scalar.copy)
        round_hidden(1, nc.vector.tensor_copy)
        round_hidden(2, nc.scalar.copy)
        round_hidden(3, nc.scalar.copy)
        for c in chunks:
            quantise_hidden(c)
        adapter((0,), 0)
        adapter((1,), 0)
        adapter((0, 1), 1)
        for c in (2, 3):
            for u in range(2):
                direct((c,), u)
                adapter((c,), u)
        low, high = (0, PACK // 2), (PACK // 2, PACK)
        empty(0, 0, nc.scalar.copy)
        store(*low, places(0))
        empty(1, 0, nc.scalar.copy)
        store(*low, places(1))
        empty(0, 1, nc.vector.tensor_copy)
        empty(1, 1, nc.scalar.copy)
        store(*high, slice(0, HALF))
        round_result(0)
        empty(2, 0, nc.scalar.copy)
        empty(2, 1, nc.scalar.copy)
        round_result(1)
        empty(3, 0, nc.scalar.copy)
        store(*low, slice(HALF, S))
        empty(3, 1, nc.scalar.copy)
        store(*high, slice(HALF, S))
        round_result(2)
        quantise_result(0, 2)
        nc.sync.dma_start(out=words(out_1)[:, :HALF], in_=y_codes[:, :HALF].bitcast(I32))
        round_result(3)
        quantise_result(2, 3)
        quantise_result(3, 4)
        nc.sync.dma_start(out=words(out_1)[:, HALF:], in_=y_codes[:, HALF:].bitcast(I32))
        for g in range(P // QUADRANT):
            queue = nc.sync if g % 2 == 0 else nc.scalar
            queue.dma_start(
                out=out_2[0][PACK * g : PACK * (g + 1), :].bitcast(I32),
                in_=y_plane[QUADRANT * g : QUADRANT * g + PACK, :].bitcast(I32),
            )
